import numpy as np
import ml_dtypes


def mxq(x, axis, fmt="e4m3"):
    dtype, down = {"e4m3": (ml_dtypes.float8_e4m3fn, 7), "e5m2": (ml_dtypes.float8_e5m2, 14)}[fmt]
    v = np.moveaxis(np.asarray(x, np.float32).astype(ml_dtypes.bfloat16).astype(np.float64), axis, -1)
    blocks = v.reshape(v.shape[:-1] + (-1, 32))
    amax = np.abs(blocks).max(-1, keepdims=True)
    byte = np.maximum(np.where(amax > 0, np.frexp(amax)[1] - 1 + 127, 0) - down, 1)
    scale = np.exp2(byte - 127.0)
    codes = (blocks / scale).astype(np.float32).astype(dtype).astype(np.float64)
    return np.moveaxis((codes * scale).reshape(v.shape), -1, axis)


WIDE = False


def mx_kscale(k):
    if not WIDE:
        return np.ones(k)
    levels = np.array([10, -10, 5, -5, 0])
    if k % 512:
        return np.exp2(np.random.permutation(np.resize(levels, k // 32))).repeat(32)
    a = np.empty((k // 512, 16))
    for p in range(k // 512):
        a[p, :8] = np.random.permutation(np.resize(levels, 8))
        for g in range(8):
            far = levels[np.abs(levels - a[p, g]) >= 10]
            a[p, g + 8] = far[np.random.randint(len(far))]
    return np.exp2(a.ravel()).repeat(32)


BF16 = ml_dtypes.bfloat16


def bf(x):
    return np.asarray(x, np.float32).astype(BF16)


def f64(x):
    return np.asarray(x).astype(np.float64)


E2M1 = np.array([0.0, 0.5, 1.0, 1.5, 2.0, 3.0, 4.0, 6.0, -0.0, -0.5, -1.0, -1.5, -2.0, -3.0, -4.0, -6.0])


def pack_weight(w, fmt):
    k, n = w.shape
    w = f64(bf(w)).reshape(k // 32, 32, n)
    amax = np.abs(w).max(1)
    if fmt == "e4m3":
        byte = np.frexp(amax)[1] - 1 + 127 - 7
    else:
        mant, ex = np.frexp(amax / 6.0)
        byte = np.where(mant > 0.5, ex, ex - 1) + 127
    byte = np.clip(np.where(amax > 0, byte, 1), 1, 254)
    scaled = (w * np.exp2(127.0 - byte)[:, None, :]).reshape(k, n).astype(np.float32)
    by_word = np.ascontiguousarray(scaled.reshape(k // 512, 128, 4, n).transpose(0, 1, 3, 2))
    if fmt == "e4m3":
        words = by_word.astype(ml_dtypes.float8_e4m3fn).view(np.uint8)
    else:
        c = by_word.astype(ml_dtypes.float4_e2m1fn).view(np.uint8) & 0xF
        words = c[..., 0::2] | (c[..., 1::2] << 4)
    return np.ascontiguousarray(words), np.ascontiguousarray(byte.astype(np.uint8).reshape(k // 512, 16, n))


def unpack_weight(words, scales, fmt):
    g, p, n, _ = words.shape
    if fmt == "e4m3":
        vals = np.ascontiguousarray(words).view(ml_dtypes.float8_e4m3fn).astype(np.float64)
    else:
        nib = np.empty((g, p, n, 4), np.uint8)
        nib[..., 0::2] = words & 0xF
        nib[..., 1::2] = words >> 4
        vals = E2M1[nib]
    vals = vals * np.repeat(np.exp2(scales.astype(np.float64) - 127.0), 8, axis=1)[..., None]
    return vals.transpose(0, 1, 3, 2).reshape(g * 512, n)
def pack4(w):
    words, scales = pack_weight(w, "e2m1")
    return words.reshape(words.shape[0], 128, -1), scales


def unpack4(words, scales):
    return unpack_weight(words.reshape(words.shape[0], 128, -1, 2), scales, "e2m1")


def planes(Y):
    n, m = Y.shape
    b = f64(bf(Y)).reshape(n // 32, 32, m)
    amax = np.abs(b).max(1)
    byte = np.clip(np.where(amax > 0, np.frexp(amax)[1] - 1 + 127 - 7, 1), 1, 254)
    codes = (b * np.exp2(127.0 - byte)[:, None, :]).reshape(n, m).astype(np.float32).astype(ml_dtypes.float8_e4m3fn).view(np.uint8)
    words = codes.reshape(n // 512, 128, 4, m).transpose(0, 1, 3, 2)
    return np.ascontiguousarray(words), np.ascontiguousarray(byte.astype(np.uint8).reshape(n // 512, 16, m))


S, D = 512, 1024

def setup_inputs():
    s = mx_kscale(D)[:, None]
    t = mx_kscale(D)
    xr_words, xr_scales = pack_weight(np.random.randn(D, S) * s, "e4m3")
    xi_words, xi_scales = pack_weight(np.random.randn(D, S) * s, "e4m3")
    ar_words, ar_scales = pack4(np.random.randn(D, D) / np.sqrt(2 * D) / s)
    ai_words, ai_scales = pack4(np.random.randn(D, D) / np.sqrt(2 * D) / s)
    angle = 2 * np.pi * np.random.rand(D)
    size = np.exp(0.4 * np.random.randn(D)) / (2 * np.sqrt(D))
    br = np.random.randn(D, D) * size / t[:, None]
    bi = np.random.randn(D, D) * size / t[:, None]
    return {"xr_words": xr_words, "xr_scales": xr_scales, "xi_words": xi_words, "xi_scales": xi_scales,
            "ar_words": ar_words, "ar_scales": ar_scales, "ai_words": ai_words, "ai_scales": ai_scales,
            "d_re": bf(np.cos(angle) * t), "d_im": bf(np.sin(angle) * t), "br": bf(br), "bi": bf(bi)}

def reference(xr_words, xr_scales, xi_words, xi_scales, ar_words, ar_scales, ai_words, ai_scales, d_re, d_im, br, bi):
    xr = unpack_weight(xr_words, xr_scales, "e4m3").T
    xi = unpack_weight(xi_words, xi_scales, "e4m3").T
    ar, ai = unpack4(ar_words, ar_scales), unpack4(ai_words, ai_scales)
    dr, di = f64(d_re), f64(d_im)
    ur = (xr @ ar) - (xi @ ai)
    ui = (xr @ ai) + (xi @ ar)
    hr = mxq(ur * dr - ui * di, 1, "e4m3")
    hi = mxq(ur * di + ui * dr, 1, "e4m3")
    qr, qi = mxq(f64(br), 0, "e4m3"), mxq(f64(bi), 0, "e4m3")
    zr = (hr @ qr) - (hi @ qi)
    zi = (hr @ qi) + (hi @ qr)
    y = zr * zr + zi * zi
    Y = y.T
    words, scales = planes(Y)
    return y, words, scales

@@ -1,0 +1,359 @@
+from contextlib import ExitStack
+
+import concourse.mybir as mybir
+from concourse.masks import make_identity
+
+F32 = mybir.dt.float32
+BF16 = mybir.dt.bfloat16
+I32 = mybir.dt.int32
+U32 = mybir.dt.uint32
+U8 = mybir.dt.uint8
+FP8X4 = mybir.dt.float8_e4m3fn_x4
+FP4X4 = mybir.dt.float4_e2m1fn_x4
+ACT = mybir.ActivationFunctionType
+ALU = mybir.AluOpType
+
+P = 128
+S = 512
+D = 1024
+FLOPS = 8 * 2 * S * D * D
+RE, IM, NEG_IM = 0, 1, 2
+
+PROGRAM = """
+pool.za.1 pool.zx.1 dve.za.0 dve.zx.0 dve.warm dve.zd sp.lah.100123 sp.lxs.101 pool.lxs.123 sp.la.10 sp.lx2.1 sp.lah.000123 sp.la.00 sp.lx2.0 sp.lxs.00123 pool.ld.0 pool.ld.1 pool.ident sp.lb.0001 sp.lb.1001 sp.la.11 sp.la.01 sp.lah.110123 sp.lah.010123 sp.lb.0101 sp.lb.1101 sp.lb.0012 sp.lb.1012 sp.lb.0112 sp.lb.1112
+dve.as.10 dve.aw.10 pe.ii.00 pe.ii.11 dve.aw.00 act.a1.0 dve.d32 dve.as.00 pe.dt.2 act.a1.1
+pe.ii.23 dve.dc pe.rr.04 act.a1.2 pe.rr.15 dve.v1.0 pe.ir.06 dve.v1.1 pe.rr.27 act.a3.0
+dve.b.0002 pe.ii.30 act.a2.0 dve.b.0024 pe.ri.0 act.a2.1 dve.v1.2 pe.ir.11 act.a1.3 dve.v3.0
+pe.ir.22 act.b.1002 dve.bq.0002 pe.ri.1 dve.aw.11 dve.bq.0024 pe.ri.2 act.a3.1 dve.v2.0 pe.rr.33
+act.b.1024 dve.as.11 dve.v3.1 pe.ii.44 dve.v1.3 pe.ir.35 act.a2.2 dve.bq.1002 pe.ri.3 dve.v2.1
+act.a3.2 dve.as.01 pe.ii.57 act.a2.3 dve.aw.01 dve.v3.2 act.a3.3 pe.rr.40 dve.v2.2 act.a1.4
+pe.rr.56 dve.v3.3 act.a1.5 pe.ii.63 dve.v2.3 act.h.010 pe.rr.61 dve.v1.4 pe.ii.72 act.h.000
+dve.h.001 pe.ir.44 dve.v1.5 act.a3.4 dve.b.0102 pe.rr.77 act.a2.4 pe.ir.55 act.h.011 dve.bq.1024
+dve.b.0124 act.a1.6 dve.hn.00 dve.h.002 act.a2.5 dve.hq.00 dve.hn.01 act.h.003 dve.bq.0102 pe.zi.000
+dve.v1.6 act.a1.7 pe.ri.4 dve.h.012 act.a3.5 dve.hq.01 pe.ri.5 dve.hq.02 act.h.013 dve.hn.02
+pe.ir.66 dve.v1.7 act.a3.6 pe.ri.6 dve.v3.4 act.a2.6 pe.zi.103 dve.hqn.00 dve.hq.03 act.b.1102
+pe.ir.71 dve.hqn.01 dve.v2.4 pe.zi.202 dve.hqn.02 dve.v3.5 act.a2.7 pe.ri.7 dve.v2.5 act.a3.7
+pe.zr.007 dve.v3.6 act.b.1124 pe.zr.104 dve.v3.7 pe.zi.305 dve.hn.03 dve.v2.6 act.h.110 dve.v2.7
+act.b.0046 pe.zr.206 dve.bq.0124 dve.h.100 dve.hn.10 dve.h.112 act.h.111 dve.bq.1124 dve.hqn.03 act.h.101
+dve.hq.10 pe.zr.301 dve.hn.11 dve.bq.1102 act.h.103 dve.hqn.10 dve.h.102 pe.zi.01 act.b.0146 dve.hqn.11
+dve.hn.12 dve.hq.11 pe.zr.01 dve.hqn.12 dve.hq.12 pe.zr.11 act.b.1146 dve.b.1046 pe.zi.11 dve.bq.0046
+dve.bq.1046 pe.zi.21 act.sr.0 dve.bq.0146 pe.zr.21 dve.bq.1146 act.h.113 dve.b.0068 pe.zq.407 act.si.0
+dve.hq.13 act.sr.1 dve.add.0 pe.zq.500 act.b.1068 dve.hn.13 dve.bq.0068 sp.sy.0 dve.cast.0 pe.zi.31
+dve.hqn.13 dve.b.0168 act.si.1 pe.zq.604 act.sq.40 dve.b.1168 act.sr.2 dve.bq.1068 pe.zr.31 dve.add.1
+act.sq.50 pe.zq.703 dve.bq.1168 act.si.2 sp.sy.1 dve.bq.0168 act.sr.3 pe.zq.417 dve.add.2 act.si.3
+dve.addq.40 sp.sy.2 dve.addq.50 act.sq.60 pe.zq.516 dve.cast.1 dve.cast.2 act.sq.70 dve.addq.60 pe.zq.610
+act.sq.41 dve.add.3 act.sq.51 dve.cast.3 sp.sy.3 dve.addq.70 pe.turn.20 dve.addq.41 pe.turn.11 pe.turn.52
+act.rg.0 pe.turn.43 dve.cast.4 pe.zq.713 sp.sy.4 act.rg.1 dve.rg.2 act.sq.61 dve.yq.0 dve.addq.51
+act.rg.3 dve.yq.1 dve.yq.2 pe.turn.74 sp.sy.5 dve.addq.61 act.sq.71 dve.cast.5 sp.sy.6 dve.yq.3
+dve.cast.6 act.rg.4 pe.turn.65 sp.ss.0040 dve.addq.71 sp.ss.0041 sp.ss.0042 pe.turn.26 act.rg.5 dve.yq.4
+sp.sw.004 dve.cast.7 sp.sy.7 sp.ss.0043 dve.rg.6 pe.turn.17 dve.yq.5 dve.yq.6 dve.rg.7 sp.sw.103
+dve.yq.7 sp.sw.134 sp.ss.1040 sp.ss.1041 sp.ss.1042 sp.ss.1043
+"""
+
+
+def tile_complex_layers_intensity_planes_h2_kernel(
+    tc, xr_words, xr_scales, xi_words, xi_scales, ar_words, ar_scales, ai_words, ai_scales,
+    d_re, d_im, br, bi, out_0, out_1, out_2,
+):
+    nc = tc.nc
+    with ExitStack() as ctx:
+        keep = ctx.enter_context(tc.tile_pool(name="keep", bufs=1))
+        work = ctx.enter_context(tc.tile_pool(name="work", bufs=2))
+        psum = ctx.enter_context(tc.psum_pool(name="psum", bufs=1))
+        ctx.enter_context(tc.manual_schedule())
+
+        def kept(name, shape, dtype):
+            return keep.tile(shape, dtype, name=name, align_bytes=64)
+
+        def bank(n):
+            return psum.tile([P, 512], F32, name="bank%d" % n)
+
+        parts = (RE, IM)
+        x_words = [kept("x_words%d" % m, [P, 2, S], U32) for m in parts]
+        x_scales = [kept("x_scales%d" % m, [P, 2, S], U8) for m in parts]
+        a_raw = [[kept("a_raw%d%d" % (m, g), [P, 2, 1024], U8) for g in range(2)] for m in parts]
+        a_raw_scales = [kept("a_raw_scales%d" % m, [P, 2, D], U8) for m in parts]
+        a_words = [[kept("a_words%d%d" % (m, g), [P, 2, 4, 256], U8) for g in range(2)] for m in parts]
+        a_scales = [[kept("a_scales%d%d" % (m, g), [P, 2, 4, P], U8) for g in range(2)] for m in parts]
+        b_raw = [[kept("b_raw%d%d" % (m, g), [P, 4, D], BF16) for g in range(2)] for m in parts]
+        b_words = [[kept("b_words%d%d" % (m, g), [P, D], U32) for g in range(2)] for m in parts]
+        b_scales = [[kept("b_scales%d%d" % (m, g), [P, D], U8) for g in range(2)] for m in parts]
+        h_rows = [kept("h_rows%d" % g, [P, 2, 4, S], BF16) for g in range(2)]
+        h_grouped = [kept("h_grouped%d" % g, [P, 4, 3, P, 4], BF16) for g in range(2)]
+        h_words = [kept("h_words%d" % g, [P, 4, 3, P], U32) for g in range(2)]
+        h_scales = [kept("h_scales%d" % g, [P, 4, 3, P], U8) for g in range(2)]
+        y_words = [kept("y_words%d" % h, [P, S], U32) for h in range(2)]
+        y_scales = [kept("y_scales%d" % h, [P, S], U8) for h in range(2)]
+        identity = kept("identity", [P, P], F32)
+        d_rows = kept("d_rows", [P, 2, P], BF16)
+        d_rows32 = kept("d_rows32", [P, 2, P], F32)
+        d_cols = kept("d_cols", [P, 2, 12], F32)
+        warm = kept("warm", [P, 2], F32)
+
+
+        queues = {"sp": nc.sync, "act": nc.scalar, "pool": nc.gpsimd, "dve": nc.vector}
+        x_src = ((xr_words, xr_scales), (xi_words, xi_scales))
+        a_src = ((ar_words, ar_scales), (ai_words, ai_scales))
+        tiles = {}
+
+        def fast(ap_out, ap_in):
+            return (ap_out.rearrange("p (c i) t -> p c t i", i=4), ap_in.rearrange("p t (c i) -> p c t i", i=4))
+
+        def interleave(e, out, in_):
+            if e == "act":
+                nc.scalar.copy(out=out, in_=in_)
+            elif e == "dve":
+                nc.vector.tensor_copy(out=out, in_=in_)
+            else:
+                nc.gpsimd.tensor_scalar(out=out, in0=in_, scalar1=1.0, scalar2=0.0, op0=ALU.mult, op1=ALU.add)
+
+        def mm(acc, lw, ls, rw, rs, start, stop):
+            nc.tensor.matmul_mx(out=acc, lhsT=lw, lhsT_scale=ls, rhs=rw, rhs_scale=rs, start=start, stop=stop)
+
+        def first(acc, i, am, xm, start, stop):
+            g, t = divmod(i, 4)
+            for k in range(2):
+                mm(acc[:], a_words[am][g][:, k, t, :].bitcast(FP4X4), a_scales[am][g][:, k, t, :],
+                   x_words[xm][:, k, :].bitcast(FP8X4), x_scales[xm][:, k, :], start and k == 0, stop and k == 1)
+
+        def second(acc, j, cols, g, terms, start, stop):
+            rows = slice(P * j, P * (j + 1))
+            for n, (hm, bm) in enumerate(terms):
+                mm(acc, h_words[g][:, j, hm, :].bitcast(FP8X4), h_scales[g][:, j, hm, :],
+                   b_words[bm][g][:, cols].bitcast(FP8X4), b_scales[bm][g][:, cols],
+                   start and n == 0, stop and n == 1)
+
+        zr_terms = [(RE, RE), (NEG_IM, IM)]
+        zi_terms = [(RE, IM), (IM, RE)]
+
+        def step(e, kind, a):
+            eng = queues.get(e)
+            if kind == "warm":
+                nc.vector.memset(warm[:], 0.0)
+                nc.scalar.activation(out=warm[:, 1:2], in_=warm[:, 0:1], func=ACT.Square)
+            elif kind == "ident":
+                make_identity(nc, identity[:])
+            elif kind == "zd":
+                eng.memset(d_rows[:], 0.0)
+            elif kind == "ld":
+                m = a[0]
+                eng.dma_start(out=d_rows[4 * m:4 * m + 4, :, :].rearrange("t g (a c) -> t (g a) c", c=4),
+                              in_=(d_re, d_im)[m].rearrange("(a t c) -> t a c", t=4, c=4))
+            elif kind == "d32":
+                nc.vector.tensor_copy(out=d_rows32[:], in_=d_rows[:])
+            elif kind == "dt":
+                tiles["dt"] = bank(a[0])
+                for g in range(2):
+                    nc.tensor.transpose(tiles["dt"][:, P * g:P * (g + 1)], d_rows32[:, g, :], identity[:])
+            elif kind == "dc":
+                turned = tiles["dt"][:, :2 * P].rearrange("p (g c) -> p g c", g=2)
+                nc.vector.tensor_copy(out=d_cols[:, :, 0:8], in_=turned[:, :, 0:8])
+                nc.vector.tensor_scalar(out=d_cols[:, :, 8:12], in0=turned[:, :, 4:8], scalar1=-1.0, scalar2=None, op0=ALU.mult)
+            elif kind == "za":
+                eng.memset(a_raw_scales[a[0]][:].rearrange("p g n -> p (g n)").bitcast(I32), 0)
+            elif kind == "zx":
+                eng.memset(x_scales[a[0]][:].rearrange("p g n -> p (g n)").bitcast(I32), 0)
+            elif kind in ("las", "lxs"):
+                m = a[0]
+                plane, source = (a_raw_scales[m], a_src[m][1]) if kind == "las" else (x_scales[m], x_src[m][1])
+                rows = source.rearrange("g (q r) n -> r q g n", r=4)
+                for r in a[1:]:
+                    eng.dma_start(out=plane[r:P:32, :, :].bitcast(I32), in_=rows[r].bitcast(I32))
+            elif kind == "lx":
+                m, g = a
+                eng.dma_start(out=x_words[m][:, g, :].bitcast(I32),
+                              in_=x_src[m][0][g].rearrange("p n t -> p (n t)").bitcast(I32))
+            elif kind == "la":
+                m, g = a
+                eng.dma_start(out=a_raw[m][g][:].bitcast(I32),
+                              in_=a_src[m][0][:, :, 1024 * g:1024 * (g + 1)].rearrange("k p n -> p k n").bitcast(I32))
+            elif kind == "lb":
+                m, g, h0, h1 = a
+                cols = slice(512 * h0, 512 * h1)
+                rows = (br, bi)[m][512 * g:512 * (g + 1), cols].rearrange("(a t c) n -> c a t n", t=4, c=4)
+                for c in range(4):
+                    eng.dma_start(out=b_raw[m][g][c:P:4, :, cols], in_=rows[c])
+            elif kind == "lx2":
+                m = a[0]
+                eng.dma_start(out=x_words[m][:].bitcast(I32),
+                              in_=x_src[m][0].rearrange("g p n t -> p g (n t)").bitcast(I32))
+            elif kind == "lah":
+                m, h = a[0], a[1]
+                cols = slice(512 * h, 512 * (h + 1))
+                rows = a_src[m][1][:, :, cols].rearrange("g (q r) n -> r q g n", r=4)
+                for r in a[2:]:
+                    eng.dma_start(out=a_raw_scales[m][r:P:32, :, cols].bitcast(I32), in_=rows[r].bitcast(I32))
+            elif kind == "aw":
+                m, g = a
+                nc.vector.tensor_copy(
+                    out=a_words[m][g][:].bitcast(I32).rearrange("p k t (a j) -> p k t a j", j=2),
+                    in_=a_raw[m][g][:].bitcast(I32).rearrange("p k (a t j) -> p k t a j", t=4, j=2))
+            elif kind == "as":
+                m, g = a
+                nc.vector.tensor_copy(
+                    out=a_scales[m][g][:].bitcast(I32),
+                    in_=a_raw_scales[m][:, :, 512 * g:512 * (g + 1)].bitcast(I32).rearrange(
+                        "p k (a t) -> p k t a", t=4))
+            elif kind == "ii":
+                i, n = a
+                tiles["ii", i] = bank(n)
+                first(tiles["ii", i], i, IM, IM, True, True)
+            elif kind == "rr":
+                i, n = a
+                tiles["rr", i] = bank(n)
+                first(tiles["rr", i], i, RE, RE, True, True)
+            elif kind == "ir":
+                i, n = a
+                tiles["ui", i] = bank(n)
+                first(tiles["ui", i], i, IM, RE, True, False)
+            elif kind == "ri":
+                first(tiles["ui", a[0]], a[0], RE, IM, False, True)
+            elif kind == "a1":
+                tiles["ii_sb", a[0]] = work.tile([P, S], F32, name="ii_sb", bufs=4)
+                nc.scalar.copy(out=tiles["ii_sb", a[0]][:], in_=tiles["ii", a[0]][:])
+            elif kind == "v1":
+                tiles["ur", a[0]] = work.tile([P, S], F32, name="ur", bufs=3)
+                nc.vector.tensor_tensor(out=tiles["ur", a[0]][:], in0=tiles["rr", a[0]][:], in1=tiles["ii_sb", a[0]][:],
+                                        op=ALU.subtract)
+            elif kind in ("a2", "a3"):
+                i = a[0]
+                g, t = divmod(i, 4)
+                c = t if kind == "a2" else 4 + t
+                tiles[kind, i] = work.tile([P, S], F32, name="ur_" + kind, bufs=3)
+                if e == "act":
+                    nc.scalar.activation(out=tiles[kind, i][:], in_=tiles["ur", i][:], func=ACT.Copy, scale=d_cols[:, g, c:c + 1])
+                else:
+                    eng.tensor_scalar(out=tiles[kind, i][:], in0=tiles["ur", i][:], scalar1=d_cols[:, g, c:c + 1],
+                                      scalar2=0.0, op0=ALU.mult, op1=ALU.add)
+            elif kind in ("v2", "v3"):
+                i = a[0]
+                cols = slice(P * a[1], P * a[2]) if len(a) > 1 else slice(0, S)
+                g, t = divmod(i, 4)
+                m, c, other = (RE, 8 + t, "a2") if kind == "v2" else (IM, t, "a3")
+                nc.vector.scalar_tensor_tensor(out=h_rows[g][:, m, t, cols], in0=tiles["ui", i][:, cols],
+                                               scalar=d_cols[:, g, c:c + 1], in1=tiles[other, i][:, cols],
+                                               op0=ALU.mult, op1=ALU.add)
+            elif kind == "b":
+                m, g, c0, c1 = a
+                tag = "b_grouped_pool" if e == "pool" else "b_grouped"
+                grouped = work.tile([P, 128 * (c1 - c0), 4], BF16, name=tag, bufs=(1 if e == "pool" else 4), align_bytes=64)
+                tiles["b", m, g, c0] = grouped
+                interleave(e, *fast(grouped[:], b_raw[m][g][:, :, 128 * c0:128 * c1]))
+            elif kind == "bq":
+                m, g, c0, c1 = a
+                cols = slice(128 * c0, 128 * c1)
+                nc.vector.quantize_mx(out=b_words[m][g][:, cols].bitcast(FP8X4), scales=b_scales[m][g][:, cols],
+                                      in_=tiles["b", m, g, c0][:].rearrange("p n t -> p (n t)"))
+            elif kind == "h":
+                g, m, j = a
+                tiles["hg", g, j] = h_grouped[g][:, j, 0:2, :, :]
+                interleave(e, *fast(h_grouped[g][:, j, m, :, :], h_rows[g][:, m, :, P * j:P * (j + 1)]))
+            elif kind == "h2":
+                g, j = a
+                staged = work.tile([P, 2, P, 4], BF16, name="b_grouped_pool", bufs=1, align_bytes=64)
+                tiles["hg", g, j] = staged
+                interleave(e, staged[:], h_rows[g][:, :, :, P * j:P * (j + 1)].rearrange("p m t s -> p m s t"))
+            elif kind == "hn":
+                g, j = a
+                nc.vector.tensor_scalar(out=h_grouped[g][:, j, NEG_IM, :, :], in0=tiles["hg", g, j][:, IM, :, :],
+                                        scalar1=-1.0, scalar2=None, op0=ALU.mult)
+            elif kind == "hq":
+                g, j = a
+                nc.vector.quantize_mx(out=h_words[g][:, j, 0:2, :].rearrange("p m s -> p (m s)").bitcast(FP8X4),
+                                      scales=h_scales[g][:, j, 0:2, :].rearrange("p m s -> p (m s)"),
+                                      in_=tiles["hg", g, j][:].rearrange("p m s t -> p (m s t)"))
+            elif kind == "hqn":
+                g, j = a
+                nc.vector.quantize_mx(out=h_words[g][:, j, NEG_IM, :].bitcast(FP8X4), scales=h_scales[g][:, j, NEG_IM, :],
+                                      in_=h_grouped[g][:, j, NEG_IM, :, :].rearrange("p s t -> p (s t)"))
+            elif kind in ("zr", "zi"):
+                u, g = a[0], a[1]
+                h, j = divmod(u, 4)
+                if g == 0:
+                    tiles[kind, u] = bank(a[2])
+                second(tiles[kind, u][:], j, slice(512 * h, 512 * (h + 1)), g, zr_terms if kind == "zr" else zi_terms,
+                       g == 0, g == 1)
+            elif kind == "zq":
+                u, q, n = a
+                h, j = divmod(u, 4)
+                tiles["zq", u, q] = bank(n)
+                cols = slice(512 * h + 256 * q, 512 * h + 256 * (q + 1))
+                for c, terms in enumerate((zr_terms, zi_terms)):
+                    for g in range(2):
+                        second(tiles["zq", u, q][:, 256 * c:256 * (c + 1)], j, cols, g, terms, g == 0, g == 1)
+            elif kind in ("sr", "si"):
+                u = a[0]
+                if kind == "sr":
+                    tiles["sq", u] = work.tile([P, 2, 512], F32, name="sq")
+                c = 0 if kind == "sr" else 1
+                nc.scalar.activation(out=tiles["sq", u][:, c, :], in_=tiles["z" + kind[1], u][:], func=ACT.Square)
+            elif kind == "sq":
+                u, q = a
+                tiles["sq", u, q] = work.tile([P, 512], F32, name="sqq", bufs=3)
+                nc.scalar.activation(out=tiles["sq", u, q][:], in_=tiles["zq", u, q][:], func=ACT.Square)
+            elif kind == "add":
+                u = a[0]
+                tiles["y", u] = work.tile([P, 512], F32, name="y", bufs=6)
+                nc.vector.tensor_tensor(out=tiles["y", u][:], in0=tiles["sq", u][:, 0, :], in1=tiles["sq", u][:, 1, :], op=ALU.add)
+            elif kind == "addq":
+                u, q = a
+                if q == 0:
+                    tiles["y", u] = work.tile([P, 512], F32, name="y", bufs=6)
+                nc.vector.tensor_tensor(out=tiles["y", u][:, 256 * q:256 * (q + 1)], in0=tiles["sq", u, q][:, :256],
+                                        in1=tiles["sq", u, q][:, 256:], op=ALU.add)
+            elif kind == "sy":
+                u = a[0]
+                h, j = divmod(u, 4)
+                c0, c1 = (256 * a[1], 256 * a[2]) if len(a) > 1 else (0, 512)
+                eng.dma_start(out=out_0[P * j:P * (j + 1), 512 * h + c0:512 * h + c1], in_=tiles["y", u][:, c0:c1])
+            elif kind == "cast":
+                u = a[0]
+                q0, q1 = (a[1], a[2]) if len(a) > 1 else (0, 2)
+                if q0 == 0:
+                    tiles["pairs", u] = work.tile([P, 2, P, 2], BF16, name="y_pairs", bufs=8)
+                out = tiles["pairs", u][:, :, 64 * q0:64 * q1, :]
+                in_ = tiles["y", u][:, 256 * q0:256 * q1].rearrange("s (p w e) -> s w p e", w=2, e=2)
+                if e == "act":
+                    nc.scalar.copy(out=out, in_=in_)
+                else:
+                    nc.vector.tensor_copy(out=out, in_=in_)
+            elif kind == "turn":
+                n = a[0]
+                turned = bank(n)
+                for c, u in enumerate(a[1:]):
+                    tiles["turned", u] = turned[:, 2 * P * c:2 * P * (c + 1)]
+                    words = tiles["pairs", u][:].rearrange("s w p e -> s (w p e)").bitcast(F32)
+                    for w in range(2):
+                        nc.tensor.transpose(tiles["turned", u][:, P * w:P * (w + 1)], words[:, P * w:P * (w + 1)], identity[:])
+            elif kind == "rg":
+                u = a[0]
+                tiles["yg", u] = work.tile([P, P, 4], BF16, name="y_grouped", bufs=4, align_bytes=64)
+                out = tiles["yg", u][:].rearrange("p s t -> p (s t)").bitcast(F32).rearrange("p (s w) -> p s w", w=2)
+                in_ = tiles["turned", u].rearrange("p (w s) -> p s w", w=2)
+                if e == "act":
+                    nc.scalar.copy(out=out, in_=in_)
+                else:
+                    nc.vector.tensor_copy(out=out, in_=in_)
+            elif kind == "yq":
+                u = a[0]
+                h, j = divmod(u, 4)
+                cols = slice(P * j, P * (j + 1))
+                nc.vector.quantize_mx(out=y_words[h][:, cols].bitcast(FP8X4), scales=y_scales[h][:, cols],
+                                      in_=tiles["yg", u][:].rearrange("p s t -> p (s t)"))
+            elif kind == "sw":
+                h, j0, j1 = a
+                cols = slice(P * j0, P * j1)
+                eng.dma_start(out=out_1[h, :, cols, :].rearrange("p m t -> p (m t)").bitcast(I32),
+                              in_=y_words[h][:, cols].bitcast(I32))
+            elif kind == "ss":
+                h, j0, j1 = a[:3]
+                cols = slice(P * j0, P * j1)
+                rows = out_2[h].rearrange("(q r) m -> r q m", r=4)
+                for r in a[3:]:
+                    eng.dma_start(out=rows[r][:, cols].bitcast(I32), in_=y_scales[h][r:P:32, cols].bitcast(I32))
+            else:
+                raise ValueError(kind)
+
+        for item in PROGRAM.split():
+            fields = item.split(".")
+            step(fields[0], fields[1], [int(c) for c in fields[2]] if len(fields) > 2 else [])

@@ -19,35 +19,33 @@ D = 1024
 FLOPS = 8 * 2 * S * D * D
 RE, IM, NEG_IM = 0, 1, 2
 
+CHUNKS = [1,2]
+GROUPS = [[0,1],[2,3],[4,5],[6],[7]]
 PROGRAM = """
-pool.za.1 pool.zx.1 dve.za.0 dve.zx.0 dve.warm dve.zd sp.lah.100123 sp.lxs.101 pool.lxs.123 sp.la.10 sp.lx2.1 sp.lah.000123 sp.la.00 sp.lx2.0 sp.lxs.00123 pool.ld.0 pool.ld.1 pool.ident sp.lb.0001 sp.lb.1001 sp.la.11 sp.la.01 sp.lah.110123 sp.lah.010123 sp.lb.0101 sp.lb.1101 sp.lb.0012 sp.lb.1012 sp.lb.0112 sp.lb.1112
-dve.as.10 dve.aw.10 pe.ii.00 pe.ii.11 dve.aw.00 act.a1.0 dve.d32 dve.as.00 pe.dt.2 act.a1.1
-pe.ii.23 dve.dc pe.rr.04 act.a1.2 pe.rr.15 dve.v1.0 pe.ir.06 dve.v1.1 pe.rr.27 act.a3.0
-dve.b.0002 pe.ii.30 act.a2.0 dve.b.0024 pe.ri.0 act.a2.1 dve.v1.2 pe.ir.11 act.a1.3 dve.v3.0
-pe.ir.22 act.b.1002 dve.bq.0002 pe.ri.1 dve.aw.11 dve.bq.0024 pe.ri.2 act.a3.1 dve.v2.0 pe.rr.33
-act.b.1024 dve.as.11 dve.v3.1 pe.ii.44 dve.v1.3 pe.ir.35 act.a2.2 dve.bq.1002 pe.ri.3 dve.v2.1
-act.a3.2 dve.as.01 pe.ii.57 act.a2.3 dve.aw.01 dve.v3.2 act.a3.3 pe.rr.40 dve.v2.2 act.a1.4
-pe.rr.56 dve.v3.3 act.a1.5 pe.ii.63 dve.v2.3 act.h.010 pe.rr.61 dve.v1.4 pe.ii.72 act.h.000
-dve.h.001 pe.ir.44 dve.v1.5 act.a3.4 dve.b.0102 pe.rr.77 act.a2.4 pe.ir.55 act.h.011 dve.bq.1024
-dve.b.0124 act.a1.6 dve.hn.00 dve.h.002 act.a2.5 dve.hq.00 dve.hn.01 act.h.003 dve.bq.0102 pe.zi.000
-dve.v1.6 act.a1.7 pe.ri.4 dve.h.012 act.a3.5 dve.hq.01 pe.ri.5 dve.hq.02 act.h.013 dve.hn.02
-pe.ir.66 dve.v1.7 act.a3.6 pe.ri.6 dve.v3.4 act.a2.6 pe.zi.103 dve.hqn.00 dve.hq.03 act.b.1102
-pe.ir.71 dve.hqn.01 dve.v2.4 pe.zi.202 dve.hqn.02 dve.v3.5 act.a2.7 pe.ri.7 dve.v2.5 act.a3.7
-pe.zr.007 dve.v3.6 act.b.1124 pe.zr.104 dve.v3.7 pe.zi.305 dve.hn.03 dve.v2.6 act.h.110 dve.v2.7
-act.b.0046 pe.zr.206 dve.bq.0124 dve.h.100 dve.hn.10 dve.h.112 act.h.111 dve.bq.1124 dve.hqn.03 act.h.101
-dve.hq.10 pe.zr.301 dve.hn.11 dve.bq.1102 act.h.103 dve.hqn.10 dve.h.102 pe.zi.01 act.b.0146 dve.hqn.11
-dve.hn.12 dve.hq.11 pe.zr.01 dve.hqn.12 dve.hq.12 pe.zr.11 act.b.1146 dve.b.1046 pe.zi.11 dve.bq.0046
-dve.bq.1046 pe.zi.21 act.sr.0 dve.bq.0146 pe.zr.21 dve.bq.1146 act.h.113 dve.b.0068 pe.zq.407 act.si.0
-dve.hq.13 act.sr.1 dve.add.0 pe.zq.500 act.b.1068 dve.hn.13 dve.bq.0068 sp.sy.0 dve.cast.0 pe.zi.31
-dve.hqn.13 dve.b.0168 act.si.1 pe.zq.604 act.sq.40 dve.b.1168 act.sr.2 dve.bq.1068 pe.zr.31 dve.add.1
-act.sq.50 pe.zq.703 dve.bq.1168 act.si.2 sp.sy.1 dve.bq.0168 act.sr.3 pe.zq.417 dve.add.2 act.si.3
-dve.addq.40 sp.sy.2 dve.addq.50 act.sq.60 pe.zq.516 dve.cast.1 dve.cast.2 act.sq.70 dve.addq.60 pe.zq.610
-act.sq.41 dve.add.3 act.sq.51 dve.cast.3 sp.sy.3 dve.addq.70 pe.turn.20 dve.addq.41 pe.turn.11 pe.turn.52
-act.rg.0 pe.turn.43 dve.cast.4 pe.zq.713 sp.sy.4 act.rg.1 dve.rg.2 act.sq.61 dve.yq.0 dve.addq.51
-act.rg.3 dve.yq.1 dve.yq.2 pe.turn.74 sp.sy.5 dve.addq.61 act.sq.71 dve.cast.5 sp.sy.6 dve.yq.3
-dve.cast.6 act.rg.4 pe.turn.65 sp.ss.0040 dve.addq.71 sp.ss.0041 sp.ss.0042 pe.turn.26 act.rg.5 dve.yq.4
-sp.sw.004 dve.cast.7 sp.sy.7 sp.ss.0043 dve.rg.6 pe.turn.17 dve.yq.5 dve.yq.6 dve.rg.7 sp.sw.103
-dve.yq.7 sp.sw.134 sp.ss.1040 sp.ss.1041 sp.ss.1042 sp.ss.1043
+pool.za.1 dve.zx.1 dve.za.0 dve.zx.0 dve.warm pool.zd pool.ld.0 pool.ld.1 pool.ident sp.las.10123 sp.lxs.101 sp.la.10 sp.lx.1 sp.lxs.123 sp.las.00123 sp.la.00 sp.lx.0 sp.lxs.00123 sp.lb.0001 sp.lb.1001 sp.la.11 sp.la.01 sp.lb.0101 sp.lb.1101 sp.lb.0012 sp.lb.1012 sp.lb.0112 sp.lb.1112
+dve.aw.10 dve.as.10 pe.ii.00 pe.ii.11 dve.as.00 act.a1.0 dve.as.11 pe.ii.22 dve.aw.00 act.a1.1
+dve.d32 dve.as.01 pe.dt.3 act.a1.2 pe.ii.34 dve.dc pe.rr.05 act.a1.3 pe.rr.16 dve.v1.0
+pe.rr.27 dve.v1.1 pe.ir.00 act.a3.0 dve.v1.2 pe.ri.0 act.a2.0 dve.b.0000 pe.rr.31 act.a2.1
+dve.v2.0 pe.ir.12 act.a2.2 dve.b.0001 pe.ir.23 act.a3.1 pe.ri.1 dve.v3.0 act.b.1000 pe.ir.34
+dve.aw.11 dve.v1.3 pe.ri.2 act.a3.2 dve.aw.01 pe.ir.45 act.a3.3 dve.v2.1 pe.ii.46 act.a2.3
+dve.v3.1 pe.rr.47 act.a1.4 dve.bq.000 pe.rr.50 act.b.1001 dve.v3.2 pe.ii.51 dve.v2.2 pe.rr.62
+act.a1.5 dve.v1.4 pe.ir.56 act.b.0101 dve.bq.100 pe.ri.3 pe.ii.63 dve.b.0100 act.a2.4 pe.ri.4
+dve.v1.5 act.a3.4 pe.ii.71 dve.v3.3 act.a1.6 pe.ri.5 dve.v2.3 act.h.0011 pe.ir.67 dve.h.0010
+pe.ir.70 dve.v1.6 pe.rr.73 act.a3.5 dve.h.0000 pe.ri.6 act.a1.7 dve.hn.00 pe.ri.7 act.h.0001
+dve.v3.4 dve.hqn.00 act.a2.5 dve.hq.00 act.a3.6 act.b.1100 dve.v1.7 pe.zi.004 dve.v3.5 act.a2.6
+dve.v2.4 act.a3.7 pe.zi.102 dve.v3.6 act.a2.7 pe.zi.201 dve.v2.5 act.b.0010 pe.zr.003 dve.v3.7
+pe.zr.105 dve.v2.6 act.h.1010 pe.zr.206 dve.v2.7 pe.zi.307 dve.b.1101 act.h.1000 pe.zr.300 dve.bq.010
+dve.bq.110 act.b.0011 dve.hq.10 dve.hn.10 act.h.1100 pe.zi.01 dve.h.1110 pe.zi.11 dve.hqn.10 act.b.1011
+dve.hn.11 pe.zr.01 dve.hq.11 pe.zr.11 dve.b.1010 act.sr.0 pe.zi.21 dve.hqn.11 act.sr.1 pe.zi.31
+dve.bq.001 act.si.0 pe.zr.21 dve.bq.101 act.si.1 pe.zr.31 dve.b.0110 act.sr.2 pe.zr.403 dve.b.0111
+act.b.1110 pe.zr.505 dve.b.1111 pe.zi.404 dve.bq.011 act.sr.3 pe.zi.502 pe.zi.606 act.si.2 dve.bq.111
+pe.zr.600 act.si.3 dve.add.0 pe.zi.41 pe.zr.41 dve.cast.0 act.si.4 sp.sy.0 pe.zi.51 dve.add.1
+act.sr.4 pe.zr.51 act.si.5 pe.zi.701 act.sr.5 pe.zr.61 dve.cast.1 sp.sy.1 pe.zi.61 dve.add.2
+act.sr.6 pe.turn.70 act.si.6 pe.turn.41 pe.zi.71 act.rg.0 dve.cast.2 sp.sy.2 pe.zr.703 act.rg.1
+dve.add.3 pe.zr.71 act.si.7 dve.yq.0 pe.turn.22 dve.yq.1 act.sr.7 dve.cast.3 sp.sw.004 sp.sy.3
+sp.ss.0040 act.rg.2 sp.ss.0041 pe.turn.53 sp.ss.0042 dve.add.4 act.rg.3 dve.cast.4 sp.sy.4 dve.yq.2
+pe.turn.04 dve.yq.3 dve.rg.4 sp.sw.103 sp.ss.0043 dve.yq.4 sp.sw.134 sp.ss.1040 sp.ss.1041 sp.ss.1042
+sp.ss.1043
 """
 
 
@@ -79,9 +77,9 @@ def tile_complex_layers_intensity_planes_h2_kernel(
         b_words = [[kept("b_words%d%d" % (m, g), [P, D], U32) for g in range(2)] for m in parts]
         b_scales = [[kept("b_scales%d%d" % (m, g), [P, D], U8) for g in range(2)] for m in parts]
         h_rows = [kept("h_rows%d" % g, [P, 2, 4, S], BF16) for g in range(2)]
-        h_grouped = [kept("h_grouped%d" % g, [P, 4, 3, P, 4], BF16) for g in range(2)]
-        h_words = [kept("h_words%d" % g, [P, 4, 3, P], U32) for g in range(2)]
-        h_scales = [kept("h_scales%d" % g, [P, 4, 3, P], U8) for g in range(2)]
+        h_grouped = [kept("h_grouped%d" % g, [P, CHUNKS[g], 3, S // CHUNKS[g], 4], BF16) for g in range(2)]
+        h_words = [kept("h_words%d" % g, [P, CHUNKS[g], 3, S // CHUNKS[g]], U32) for g in range(2)]
+        h_scales = [kept("h_scales%d" % g, [P, CHUNKS[g], 3, S // CHUNKS[g]], U8) for g in range(2)]
         y_words = [kept("y_words%d" % h, [P, S], U32) for h in range(2)]
         y_scales = [kept("y_scales%d" % h, [P, S], U8) for h in range(2)]
         identity = kept("identity", [P, P], F32)
@@ -90,16 +88,12 @@ def tile_complex_layers_intensity_planes_h2_kernel(
         d_cols = kept("d_cols", [P, 2, 12], F32)
         warm = kept("warm", [P, 2], F32)
 
-
         queues = {"sp": nc.sync, "act": nc.scalar, "pool": nc.gpsimd, "dve": nc.vector}
         x_src = ((xr_words, xr_scales), (xi_words, xi_scales))
         a_src = ((ar_words, ar_scales), (ai_words, ai_scales))
         tiles = {}
 
-        def fast(ap_out, ap_in):
-            return (ap_out.rearrange("p (c i) t -> p c t i", i=4), ap_in.rearrange("p t (c i) -> p c t i", i=4))
-
-        def interleave(e, out, in_):
+        def move(e, out, in_):
             if e == "act":
                 nc.scalar.copy(out=out, in_=in_)
             elif e == "dve":
@@ -107,24 +101,34 @@ def tile_complex_layers_intensity_planes_h2_kernel(
             else:
                 nc.gpsimd.tensor_scalar(out=out, in0=in_, scalar1=1.0, scalar2=0.0, op0=ALU.mult, op1=ALU.add)
 
-        def mm(acc, lw, ls, rw, rs, start, stop):
-            nc.tensor.matmul_mx(out=acc, lhsT=lw, lhsT_scale=ls, rhs=rw, rhs_scale=rs, start=start, stop=stop)
+        def interleave(e, out, in_):
+            move(e, out.rearrange("p (c i) t -> p c t i", i=4), in_.rearrange("p t (c i) -> p c t i", i=4))
+
+        def quantize(words, scales, values):
+            nc.vector.quantize_mx(out=words.bitcast(FP8X4), scales=scales, in_=values)
 
         def first(acc, i, am, xm, start, stop):
             g, t = divmod(i, 4)
             for k in range(2):
-                mm(acc[:], a_words[am][g][:, k, t, :].bitcast(FP4X4), a_scales[am][g][:, k, t, :],
-                   x_words[xm][:, k, :].bitcast(FP8X4), x_scales[xm][:, k, :], start and k == 0, stop and k == 1)
+                nc.tensor.matmul_mx(
+                    out=acc[:], lhsT=a_words[am][g][:, k, t, :].bitcast(FP4X4), lhsT_scale=a_scales[am][g][:, k, t, :],
+                    rhs=x_words[xm][:, k, :].bitcast(FP8X4), rhs_scale=x_scales[xm][:, k, :],
+                    start=start and k == 0, stop=stop and k == 1)
 
-        def second(acc, j, cols, g, terms, start, stop):
-            rows = slice(P * j, P * (j + 1))
+        def second(acc, u, g, terms):
+            h, j = divmod(u, 4)
+            c, first_row = divmod(P * j, S // CHUNKS[g])
+            rows = slice(first_row, first_row + P)
+            cols = slice(512 * h, 512 * (h + 1))
             for n, (hm, bm) in enumerate(terms):
-                mm(acc, h_words[g][:, j, hm, :].bitcast(FP8X4), h_scales[g][:, j, hm, :],
-                   b_words[bm][g][:, cols].bitcast(FP8X4), b_scales[bm][g][:, cols],
-                   start and n == 0, stop and n == 1)
+                nc.tensor.matmul_mx(
+                    out=acc[:], lhsT=h_words[g][:, c, hm, rows].bitcast(FP8X4), lhsT_scale=h_scales[g][:, c, hm, rows],
+                    rhs=b_words[bm][g][:, cols].bitcast(FP8X4), rhs_scale=b_scales[bm][g][:, cols],
+                    start=g == 0 and n == 0, stop=g == 1 and n == 1)
 
-        zr_terms = [(RE, RE), (NEG_IM, IM)]
-        zi_terms = [(RE, IM), (IM, RE)]
+        def group_of(u):
+            n = [u in units for units in GROUPS].index(True)
+            return n, u - GROUPS[n][0]
 
         def step(e, kind, a):
             eng = queues.get(e)
@@ -160,9 +164,9 @@ def tile_complex_layers_intensity_planes_h2_kernel(
                 for r in a[1:]:
                     eng.dma_start(out=plane[r:P:32, :, :].bitcast(I32), in_=rows[r].bitcast(I32))
             elif kind == "lx":
-                m, g = a
-                eng.dma_start(out=x_words[m][:, g, :].bitcast(I32),
-                              in_=x_src[m][0][g].rearrange("p n t -> p (n t)").bitcast(I32))
+                m = a[0]
+                eng.dma_start(out=x_words[m][:].bitcast(I32),
+                              in_=x_src[m][0].rearrange("g p n t -> p g (n t)").bitcast(I32))
             elif kind == "la":
                 m, g = a
                 eng.dma_start(out=a_raw[m][g][:].bitcast(I32),
@@ -173,16 +177,6 @@ def tile_complex_layers_intensity_planes_h2_kernel(
                 rows = (br, bi)[m][512 * g:512 * (g + 1), cols].rearrange("(a t c) n -> c a t n", t=4, c=4)
                 for c in range(4):
                     eng.dma_start(out=b_raw[m][g][c:P:4, :, cols], in_=rows[c])
-            elif kind == "lx2":
-                m = a[0]
-                eng.dma_start(out=x_words[m][:].bitcast(I32),
-                              in_=x_src[m][0].rearrange("g p n t -> p g (n t)").bitcast(I32))
-            elif kind == "lah":
-                m, h = a[0], a[1]
-                cols = slice(512 * h, 512 * (h + 1))
-                rows = a_src[m][1][:, :, cols].rearrange("g (q r) n -> r q g n", r=4)
-                for r in a[2:]:
-                    eng.dma_start(out=a_raw_scales[m][r:P:32, :, cols].bitcast(I32), in_=rows[r].bitcast(I32))
             elif kind == "aw":
                 m, g = a
                 nc.vector.tensor_copy(
@@ -192,22 +186,13 @@ def tile_complex_layers_intensity_planes_h2_kernel(
                 m, g = a
                 nc.vector.tensor_copy(
                     out=a_scales[m][g][:].bitcast(I32),
-                    in_=a_raw_scales[m][:, :, 512 * g:512 * (g + 1)].bitcast(I32).rearrange(
-                        "p k (a t) -> p k t a", t=4))
-            elif kind == "ii":
+                    in_=a_raw_scales[m][:, :, 512 * g:512 * (g + 1)].bitcast(I32).rearrange("p k (a t) -> p k t a", t=4))
+            elif kind in ("ii", "rr", "ir"):
                 i, n = a
-                tiles["ii", i] = bank(n)
-                first(tiles["ii", i], i, IM, IM, True, True)
-            elif kind == "rr":
-                i, n = a
-                tiles["rr", i] = bank(n)
-                first(tiles["rr", i], i, RE, RE, True, True)
-            elif kind == "ir":
-                i, n = a
-                tiles["ui", i] = bank(n)
-                first(tiles["ui", i], i, IM, RE, True, False)
+                tiles[kind, i] = bank(n)
+                first(tiles[kind, i], i, RE if kind == "rr" else IM, IM if kind == "ii" else RE, True, kind != "ir")
             elif kind == "ri":
-                first(tiles["ui", a[0]], a[0], RE, IM, False, True)
+                first(tiles["ir", a[0]], a[0], RE, IM, False, True)
             elif kind == "a1":
                 tiles["ii_sb", a[0]] = work.tile([P, S], F32, name="ii_sb", bufs=4)
                 nc.scalar.copy(out=tiles["ii_sb", a[0]][:], in_=tiles["ii", a[0]][:])
@@ -220,126 +205,84 @@ def tile_complex_layers_intensity_planes_h2_kernel(
                 g, t = divmod(i, 4)
                 c = t if kind == "a2" else 4 + t
                 tiles[kind, i] = work.tile([P, S], F32, name="ur_" + kind, bufs=3)
-                if e == "act":
-                    nc.scalar.activation(out=tiles[kind, i][:], in_=tiles["ur", i][:], func=ACT.Copy, scale=d_cols[:, g, c:c + 1])
-                else:
-                    eng.tensor_scalar(out=tiles[kind, i][:], in0=tiles["ur", i][:], scalar1=d_cols[:, g, c:c + 1],
-                                      scalar2=0.0, op0=ALU.mult, op1=ALU.add)
+                nc.scalar.activation(out=tiles[kind, i][:], in_=tiles["ur", i][:], func=ACT.Copy, scale=d_cols[:, g, c:c + 1])
             elif kind in ("v2", "v3"):
                 i = a[0]
-                cols = slice(P * a[1], P * a[2]) if len(a) > 1 else slice(0, S)
                 g, t = divmod(i, 4)
                 m, c, other = (RE, 8 + t, "a2") if kind == "v2" else (IM, t, "a3")
-                nc.vector.scalar_tensor_tensor(out=h_rows[g][:, m, t, cols], in0=tiles["ui", i][:, cols],
-                                               scalar=d_cols[:, g, c:c + 1], in1=tiles[other, i][:, cols],
+                nc.vector.scalar_tensor_tensor(out=h_rows[g][:, m, t, :], in0=tiles["ir", i][:],
+                                               scalar=d_cols[:, g, c:c + 1], in1=tiles[other, i][:],
                                                op0=ALU.mult, op1=ALU.add)
             elif kind == "b":
-                m, g, c0, c1 = a
-                tag = "b_grouped_pool" if e == "pool" else "b_grouped"
-                grouped = work.tile([P, 128 * (c1 - c0), 4], BF16, name=tag, bufs=(1 if e == "pool" else 4), align_bytes=64)
-                tiles["b", m, g, c0] = grouped
-                interleave(e, *fast(grouped[:], b_raw[m][g][:, :, 128 * c0:128 * c1]))
+                m, g, h, q = a
+                if ("b", m, g, h) not in tiles:
+                    tiles["b", m, g, h] = work.tile([P, 512, 4], BF16, name="b_grouped", bufs=3, align_bytes=64)
+                c0 = 512 * h + 256 * q
+                interleave(e, tiles["b", m, g, h][:, 256 * q:256 * (q + 1), :], b_raw[m][g][:, :, c0:c0 + 256])
             elif kind == "bq":
-                m, g, c0, c1 = a
-                cols = slice(128 * c0, 128 * c1)
-                nc.vector.quantize_mx(out=b_words[m][g][:, cols].bitcast(FP8X4), scales=b_scales[m][g][:, cols],
-                                      in_=tiles["b", m, g, c0][:].rearrange("p n t -> p (n t)"))
+                m, g, h = a
+                cols = slice(512 * h, 512 * (h + 1))
+                quantize(b_words[m][g][:, cols], b_scales[m][g][:, cols], tiles["b", m, g, h][:].rearrange("p n t -> p (n t)"))
             elif kind == "h":
-                g, m, j = a
-                tiles["hg", g, j] = h_grouped[g][:, j, 0:2, :, :]
-                interleave(e, *fast(h_grouped[g][:, j, m, :, :], h_rows[g][:, m, :, P * j:P * (j + 1)]))
-            elif kind == "h2":
-                g, j = a
-                staged = work.tile([P, 2, P, 4], BF16, name="b_grouped_pool", bufs=1, align_bytes=64)
-                tiles["hg", g, j] = staged
-                interleave(e, staged[:], h_rows[g][:, :, :, P * j:P * (j + 1)].rearrange("p m t s -> p m s t"))
+                g, c, m, q = a
+                width = min(256, S // CHUNKS[g])
+                s0 = c * (S // CHUNKS[g]) + width * q
+                interleave(e, h_grouped[g][:, c, m, width * q:width * (q + 1), :], h_rows[g][:, m, :, s0:s0 + width])
             elif kind == "hn":
-                g, j = a
-                nc.vector.tensor_scalar(out=h_grouped[g][:, j, NEG_IM, :, :], in0=tiles["hg", g, j][:, IM, :, :],
+                g, c = a
+                nc.vector.tensor_scalar(out=h_grouped[g][:, c, NEG_IM, :, :], in0=h_grouped[g][:, c, IM, :, :],
                                         scalar1=-1.0, scalar2=None, op0=ALU.mult)
             elif kind == "hq":
-                g, j = a
-                nc.vector.quantize_mx(out=h_words[g][:, j, 0:2, :].rearrange("p m s -> p (m s)").bitcast(FP8X4),
-                                      scales=h_scales[g][:, j, 0:2, :].rearrange("p m s -> p (m s)"),
-                                      in_=tiles["hg", g, j][:].rearrange("p m s t -> p (m s t)"))
+                g, c = a
+                quantize(h_words[g][:, c, 0:2, :].rearrange("p m s -> p (m s)"),
+                         h_scales[g][:, c, 0:2, :].rearrange("p m s -> p (m s)"),
+                         h_grouped[g][:, c, 0:2, :, :].rearrange("p m s t -> p (m s t)"))
             elif kind == "hqn":
-                g, j = a
-                nc.vector.quantize_mx(out=h_words[g][:, j, NEG_IM, :].bitcast(FP8X4), scales=h_scales[g][:, j, NEG_IM, :],
-                                      in_=h_grouped[g][:, j, NEG_IM, :, :].rearrange("p s t -> p (s t)"))
+                g, c = a
+                quantize(h_words[g][:, c, NEG_IM, :], h_scales[g][:, c, NEG_IM, :],
+                         h_grouped[g][:, c, NEG_IM, :, :].rearrange("p s t -> p (s t)"))
             elif kind in ("zr", "zi"):
                 u, g = a[0], a[1]
-                h, j = divmod(u, 4)
                 if g == 0:
                     tiles[kind, u] = bank(a[2])
-                second(tiles[kind, u][:], j, slice(512 * h, 512 * (h + 1)), g, zr_terms if kind == "zr" else zi_terms,
-                       g == 0, g == 1)
-            elif kind == "zq":
-                u, q, n = a
-                h, j = divmod(u, 4)
-                tiles["zq", u, q] = bank(n)
-                cols = slice(512 * h + 256 * q, 512 * h + 256 * (q + 1))
-                for c, terms in enumerate((zr_terms, zi_terms)):
-                    for g in range(2):
-                        second(tiles["zq", u, q][:, 256 * c:256 * (c + 1)], j, cols, g, terms, g == 0, g == 1)
+                second(tiles[kind, u], u, g, [(RE, RE), (NEG_IM, IM)] if kind == "zr" else [(RE, IM), (IM, RE)])
             elif kind in ("sr", "si"):
-                u = a[0]
-                if kind == "sr":
-                    tiles["sq", u] = work.tile([P, 2, 512], F32, name="sq")
-                c = 0 if kind == "sr" else 1
-                nc.scalar.activation(out=tiles["sq", u][:, c, :], in_=tiles["z" + kind[1], u][:], func=ACT.Square)
-            elif kind == "sq":
-                u, q = a
-                tiles["sq", u, q] = work.tile([P, 512], F32, name="sqq", bufs=3)
-                nc.scalar.activation(out=tiles["sq", u, q][:], in_=tiles["zq", u, q][:], func=ACT.Square)
+                n, place = group_of(a[0])
+                if ("sq", n) not in tiles:
+                    tiles["sq", n] = work.tile([P, len(GROUPS[n]), 2, 512], F32, name="sq", bufs=2)
+                nc.scalar.activation(out=tiles["sq", n][:, place, 0 if kind == "sr" else 1, :],
+                                     in_=tiles["z" + kind[1], a[0]][:], func=ACT.Square)
             elif kind == "add":
-                u = a[0]
-                tiles["y", u] = work.tile([P, 512], F32, name="y", bufs=6)
-                nc.vector.tensor_tensor(out=tiles["y", u][:], in0=tiles["sq", u][:, 0, :], in1=tiles["sq", u][:, 1, :], op=ALU.add)
-            elif kind == "addq":
-                u, q = a
-                if q == 0:
-                    tiles["y", u] = work.tile([P, 512], F32, name="y", bufs=6)
-                nc.vector.tensor_tensor(out=tiles["y", u][:, 256 * q:256 * (q + 1)], in0=tiles["sq", u, q][:, :256],
-                                        in1=tiles["sq", u, q][:, 256:], op=ALU.add)
-            elif kind == "sy":
-                u = a[0]
-                h, j = divmod(u, 4)
-                c0, c1 = (256 * a[1], 256 * a[2]) if len(a) > 1 else (0, 512)
-                eng.dma_start(out=out_0[P * j:P * (j + 1), 512 * h + c0:512 * h + c1], in_=tiles["y", u][:, c0:c1])
-            elif kind == "cast":
-                u = a[0]
-                q0, q1 = (a[1], a[2]) if len(a) > 1 else (0, 2)
-                if q0 == 0:
-                    tiles["pairs", u] = work.tile([P, 2, P, 2], BF16, name="y_pairs", bufs=8)
-                out = tiles["pairs", u][:, :, 64 * q0:64 * q1, :]
-                in_ = tiles["y", u][:, 256 * q0:256 * q1].rearrange("s (p w e) -> s w p e", w=2, e=2)
-                if e == "act":
-                    nc.scalar.copy(out=out, in_=in_)
-                else:
-                    nc.vector.tensor_copy(out=out, in_=in_)
-            elif kind == "turn":
                 n = a[0]
-                turned = bank(n)
-                for c, u in enumerate(a[1:]):
-                    tiles["turned", u] = turned[:, 2 * P * c:2 * P * (c + 1)]
-                    words = tiles["pairs", u][:].rearrange("s w p e -> s (w p e)").bitcast(F32)
-                    for w in range(2):
-                        nc.tensor.transpose(tiles["turned", u][:, P * w:P * (w + 1)], words[:, P * w:P * (w + 1)], identity[:])
+                tiles["y", n] = work.tile([P, len(GROUPS[n]), 512], F32, name="y", bufs=3)
+                nc.vector.tensor_tensor(out=tiles["y", n][:], in0=tiles["sq", n][:, :, 0, :], in1=tiles["sq", n][:, :, 1, :],
+                                        op=ALU.add)
+            elif kind == "sy":
+                n = a[0]
+                h, j = divmod(GROUPS[n][0], 4)
+                rows = out_0[P * j:P * (j + len(GROUPS[n])), 512 * h:512 * (h + 1)]
+                eng.dma_start(out=rows.rearrange("(u s) n -> s u n", s=P), in_=tiles["y", n][:])
+            elif kind == "cast":
+                n = a[0]
+                tiles["pairs", n] = work.tile([P, len(GROUPS[n]), 2, P, 2], BF16, name="y_pairs", bufs=3)
+                move(e, tiles["pairs", n][:], tiles["y", n][:].rearrange("s u (p w e) -> s u w p e", w=2, e=2))
+            elif kind == "turn":
+                n = a[1]
+                tiles["turned", n] = bank(a[0])
+                words = tiles["pairs", n][:].rearrange("s u w p e -> s (u w p e)").bitcast(F32)
+                for c in range(2 * len(GROUPS[n])):
+                    nc.tensor.transpose(tiles["turned", n][:, P * c:P * (c + 1)], words[:, P * c:P * (c + 1)], identity[:])
             elif kind == "rg":
-                u = a[0]
-                tiles["yg", u] = work.tile([P, P, 4], BF16, name="y_grouped", bufs=4, align_bytes=64)
-                out = tiles["yg", u][:].rearrange("p s t -> p (s t)").bitcast(F32).rearrange("p (s w) -> p s w", w=2)
-                in_ = tiles["turned", u].rearrange("p (w s) -> p s w", w=2)
-                if e == "act":
-                    nc.scalar.copy(out=out, in_=in_)
-                else:
-                    nc.vector.tensor_copy(out=out, in_=in_)
+                n = a[0]
+                count = len(GROUPS[n])
+                tiles["yg", n] = work.tile([P, count * P * 4], BF16, name="y_grouped", bufs=3, align_bytes=64)
+                move(e, tiles["yg", n][:].bitcast(F32).rearrange("p (u s w) -> p u s w", w=2, s=P),
+                     tiles["turned", n][:, :2 * P * count].rearrange("p (u w s) -> p u s w", w=2, s=P))
             elif kind == "yq":
-                u = a[0]
-                h, j = divmod(u, 4)
-                cols = slice(P * j, P * (j + 1))
-                nc.vector.quantize_mx(out=y_words[h][:, cols].bitcast(FP8X4), scales=y_scales[h][:, cols],
-                                      in_=tiles["yg", u][:].rearrange("p s t -> p (s t)"))
+                n = a[0]
+                h, j = divmod(GROUPS[n][0], 4)
+                cols = slice(P * j, P * (j + len(GROUPS[n])))
+                quantize(y_words[h][:, cols], y_scales[h][:, cols], tiles["yg", n][:])
             elif kind == "sw":
                 h, j0, j1 = a
                 cols = slice(P * j0, P * j1)

@@ -102,7 +102,7 @@ def tile_complex_layers_intensity_planes_h2_kernel(
                 nc.gpsimd.tensor_scalar(out=out, in0=in_, scalar1=1.0, scalar2=0.0, op0=ALU.mult, op1=ALU.add)
 
         def interleave(e, out, in_):
-            move(e, out.rearrange("p (c i) t -> p c t i", i=4), in_.rearrange("p t (c i) -> p c t i", i=4))
+            move(e, out, in_.rearrange("p t n -> p n t"))
 
         def quantize(words, scales, values):
             nc.vector.quantize_mx(out=words.bitcast(FP8X4), scales=scales, in_=values)

@@ -17,35 +17,29 @@ P = 128
 S = 512
 D = 1024
 FLOPS = 8 * 2 * S * D * D
-RE, IM, NEG_IM = 0, 1, 2
+GROUP = 512
+PIECE = 256
+RE, IM, MINUS_IM = 0, 1, 2
 
-CHUNKS = [1,2]
-GROUPS = [[0,1],[2,3],[4,5],[6],[7]]
-PROGRAM = """
-pool.za.1 dve.zx.1 dve.za.0 dve.zx.0 dve.warm pool.zd pool.ld.0 pool.ld.1 pool.ident sp.las.10123 sp.lxs.101 sp.la.10 sp.lx.1 sp.lxs.123 sp.las.00123 sp.la.00 sp.lx.0 sp.lxs.00123 sp.lb.0001 sp.lb.1001 sp.la.11 sp.la.01 sp.lb.0101 sp.lb.1101 sp.lb.0012 sp.lb.1012 sp.lb.0112 sp.lb.1112
-dve.aw.10 dve.as.10 pe.ii.00 pe.ii.11 dve.as.00 act.a1.0 dve.as.11 pe.ii.22 dve.aw.00 act.a1.1
-dve.d32 dve.as.01 pe.dt.3 act.a1.2 pe.ii.34 dve.dc pe.rr.05 act.a1.3 pe.rr.16 dve.v1.0
-pe.rr.27 dve.v1.1 pe.ir.00 act.a3.0 dve.v1.2 pe.ri.0 act.a2.0 dve.b.0000 pe.rr.31 act.a2.1
-dve.v2.0 pe.ir.12 act.a2.2 dve.b.0001 pe.ir.23 act.a3.1 pe.ri.1 dve.v3.0 act.b.1000 pe.ir.34
-dve.aw.11 dve.v1.3 pe.ri.2 act.a3.2 dve.aw.01 pe.ir.45 act.a3.3 dve.v2.1 pe.ii.46 act.a2.3
-dve.v3.1 pe.rr.47 act.a1.4 dve.bq.000 pe.rr.50 act.b.1001 dve.v3.2 pe.ii.51 dve.v2.2 pe.rr.62
-act.a1.5 dve.v1.4 pe.ir.56 act.b.0101 dve.bq.100 pe.ri.3 pe.ii.63 dve.b.0100 act.a2.4 pe.ri.4
-dve.v1.5 act.a3.4 pe.ii.71 dve.v3.3 act.a1.6 pe.ri.5 dve.v2.3 act.h.0011 pe.ir.67 dve.h.0010
-pe.ir.70 dve.v1.6 pe.rr.73 act.a3.5 dve.h.0000 pe.ri.6 act.a1.7 dve.hn.00 pe.ri.7 act.h.0001
-dve.v3.4 dve.hqn.00 act.a2.5 dve.hq.00 act.a3.6 act.b.1100 dve.v1.7 pe.zi.004 dve.v3.5 act.a2.6
-dve.v2.4 act.a3.7 pe.zi.102 dve.v3.6 act.a2.7 pe.zi.201 dve.v2.5 act.b.0010 pe.zr.003 dve.v3.7
-pe.zr.105 dve.v2.6 act.h.1010 pe.zr.206 dve.v2.7 pe.zi.307 dve.b.1101 act.h.1000 pe.zr.300 dve.bq.010
-dve.bq.110 act.b.0011 dve.hq.10 dve.hn.10 act.h.1100 pe.zi.01 dve.h.1110 pe.zi.11 dve.hqn.10 act.b.1011
-dve.hn.11 pe.zr.01 dve.hq.11 pe.zr.11 dve.b.1010 act.sr.0 pe.zi.21 dve.hqn.11 act.sr.1 pe.zi.31
-dve.bq.001 act.si.0 pe.zr.21 dve.bq.101 act.si.1 pe.zr.31 dve.b.0110 act.sr.2 pe.zr.403 dve.b.0111
-act.b.1110 pe.zr.505 dve.b.1111 pe.zi.404 dve.bq.011 act.sr.3 pe.zi.502 pe.zi.606 act.si.2 dve.bq.111
-pe.zr.600 act.si.3 dve.add.0 pe.zi.41 pe.zr.41 dve.cast.0 act.si.4 sp.sy.0 pe.zi.51 dve.add.1
-act.sr.4 pe.zr.51 act.si.5 pe.zi.701 act.sr.5 pe.zr.61 dve.cast.1 sp.sy.1 pe.zi.61 dve.add.2
-act.sr.6 pe.turn.70 act.si.6 pe.turn.41 pe.zi.71 act.rg.0 dve.cast.2 sp.sy.2 pe.zr.703 act.rg.1
-dve.add.3 pe.zr.71 act.si.7 dve.yq.0 pe.turn.22 dve.yq.1 act.sr.7 dve.cast.3 sp.sw.004 sp.sy.3
-sp.ss.0040 act.rg.2 sp.ss.0041 pe.turn.53 sp.ss.0042 dve.add.4 act.rg.3 dve.cast.4 sp.sy.4 dve.yq.2
-pe.turn.04 dve.yq.3 dve.rg.4 sp.sw.103 sp.ss.0043 dve.yq.4 sp.sw.134 sp.ss.1040 sp.ss.1041 sp.ss.1042
-sp.ss.1043
+BATCHES = ((0, 1), (2, 3), (4, 5), (6,), (7,))
+LAST_UNIT = 7
+LAST_BATCH = len(BATCHES) - 1
+
+ORDER = """
+a_order as_order d_f32 ii as_order ii a_order ii_out ii d_turn d_out ii_out ii_out rr ii ur rr ii_out rr b_mix:G
+ur ur_di rr ur ur_dr ir ur_dr ri ur ur_dr ir b_q ur_di hi ri b_mix:G ur_di hr ir b_mix:S hr ri hi ir ur_dr
+a_order ri as_order ur_di a_order ii b_q b_mix:S as_order ii b_q hr b_mix:G rr ii_out hi ii ii_out hi ii ii_out
+ur rr hi_mix:S hr ir b_q ir b_q ur_di rr hr_mix:V ur_dr ri ur b_mix:G ii_out ri ur ur_di rr hi ur_dr ir hr_q
+hi_mix:S ir hi_q b_q zi_open negate hr_mix:G hr ur_di zi_open ur ri ur_dr hr ri ur_di negate ur_dr neg_q hr_q
+b_mix:S zr_open hi zr_open hr b_mix:S b_mix:G hi hi hi_q hi_mix:S hr zi_open neg_q b_q zr_open hr_mix:V hr_mix:S
+zi_open b_q hr_q zr_open hi_mix:S hi_q negate zi_close hr_q neg_q zi_close b_mix:V b_mix:S zr_close b_q zi_sq
+zr_close hi_q negate zr_sq zi_close b_q zi_sq neg_q zi_close b_mix:V b_mix:S zr_close b_q zr_close b_q b_mix:V
+zr_sq zi_open b_mix:V zr_sq zi_open zi_sq b_mix:V zi_open zi_sq zr_open b_q b_q zr_sq zr_open b_q b_q zr_open
+y_sum zr_close zi_close y_sum zr_close y_out zr_sq zi_close zi_sq pairs:V zr_close y_out zr_sq pairs:V zi_close
+zi_sq zr_open zr_sq y_sum y_turn zi_sq y_turn regroup:S zr_close y_sum y_out regroup:S zi_half pairs:V y_out
+zr_sq zi_half y_q half_sq y_q y_turn pairs:V half_sq scales_out half_pairs scales_out regroup:S scales_out
+y_turn codes_out half_pairs scales_out y_sum regroup:S y_turn y_q regroup:S y_out y_q y_q codes_out codes_out
+scales_out scales_out scales_out:S scales_out:S
 """
 
 
@@ -56,247 +50,350 @@ def tile_complex_layers_intensity_planes_h2_kernel(
     nc = tc.nc
     with ExitStack() as ctx:
         keep = ctx.enter_context(tc.tile_pool(name="keep", bufs=1))
-        work = ctx.enter_context(tc.tile_pool(name="work", bufs=2))
+        work = ctx.enter_context(tc.tile_pool(name="work", bufs=3))
         psum = ctx.enter_context(tc.psum_pool(name="psum", bufs=1))
         ctx.enter_context(tc.manual_schedule())
 
         def kept(name, shape, dtype):
             return keep.tile(shape, dtype, name=name, align_bytes=64)
 
-        def bank(n):
-            return psum.tile([P, 512], F32, name="bank%d" % n)
-
         parts = (RE, IM)
+        two = range(2)
+        part_groups = [(m, g) for m in parts for g in two]
+        h_pieces = [(g, c) for g in two for c in two]
+        h_keys = [(g, c, m) for g, c in h_pieces for m in (RE, IM, MINUS_IM)]
         x_words = [kept("x_words%d" % m, [P, 2, S], U32) for m in parts]
         x_scales = [kept("x_scales%d" % m, [P, 2, S], U8) for m in parts]
-        a_raw = [[kept("a_raw%d%d" % (m, g), [P, 2, 1024], U8) for g in range(2)] for m in parts]
-        a_raw_scales = [kept("a_raw_scales%d" % m, [P, 2, D], U8) for m in parts]
-        a_words = [[kept("a_words%d%d" % (m, g), [P, 2, 4, 256], U8) for g in range(2)] for m in parts]
-        a_scales = [[kept("a_scales%d%d" % (m, g), [P, 2, 4, P], U8) for g in range(2)] for m in parts]
-        b_raw = [[kept("b_raw%d%d" % (m, g), [P, 4, D], BF16) for g in range(2)] for m in parts]
-        b_words = [[kept("b_words%d%d" % (m, g), [P, D], U32) for g in range(2)] for m in parts]
-        b_scales = [[kept("b_scales%d%d" % (m, g), [P, D], U8) for g in range(2)] for m in parts]
-        h_rows = [kept("h_rows%d" % g, [P, 2, 4, S], BF16) for g in range(2)]
-        h_grouped = [kept("h_grouped%d" % g, [P, CHUNKS[g], 3, S // CHUNKS[g], 4], BF16) for g in range(2)]
-        h_words = [kept("h_words%d" % g, [P, CHUNKS[g], 3, S // CHUNKS[g]], U32) for g in range(2)]
-        h_scales = [kept("h_scales%d" % g, [P, CHUNKS[g], 3, S // CHUNKS[g]], U8) for g in range(2)]
-        y_words = [kept("y_words%d" % h, [P, S], U32) for h in range(2)]
-        y_scales = [kept("y_scales%d" % h, [P, S], U8) for h in range(2)]
+        a_loaded = {k: kept("a_loaded%d%d" % k, [P, 2, 2 * GROUP], U8) for k in part_groups}
+        a_loaded_scales = [kept("a_loaded_scales%d" % m, [P, 2, D], U8) for m in parts]
+        a_words = {k: kept("a_words%d%d" % k, [P, 2, 4, 2 * P], U8) for k in part_groups}
+        a_scales = {k: kept("a_scales%d%d" % k, [P, 2, 4, P], U8) for k in part_groups}
+        b_rows = {(m, g, h): kept("b_rows%d%d%d" % (m, g, h), [P, 4, GROUP], BF16) for m, g in part_groups for h in two}
+        b_words = {k: kept("b_words%d%d" % k, [P, D], U32) for k in part_groups}
+        b_scales = {k: kept("b_scales%d%d" % k, [P, D], U8) for k in part_groups}
+        h_rows = {k: kept("h_rows%d%d" % k, [P, 4, S], BF16) for k in part_groups}
+        h_words = {k: kept("h_words%d%d%d" % k, [P, PIECE], U32) for k in h_keys}
+        h_scales = {k: kept("h_scales%d%d%d" % k, [P, PIECE], U8) for k in h_keys}
+        y_words = [kept("y_words%d" % h, [P, S], U32) for h in two]
+        y_scales = [kept("y_scales%d" % h, [P, S], U8) for h in two]
+        identity_bf16 = kept("identity_bf16", [P, P], BF16)
         identity = kept("identity", [P, P], F32)
         d_rows = kept("d_rows", [P, 2, P], BF16)
-        d_rows32 = kept("d_rows32", [P, 2, P], F32)
-        d_cols = kept("d_cols", [P, 2, 12], F32)
-        warm = kept("warm", [P, 2], F32)
+        d_rows_f32 = kept("d_rows_f32", [P, 2, P], F32)
+        d_columns = kept("d_columns", [P, 2, 3, 4], F32)
 
-        queues = {"sp": nc.sync, "act": nc.scalar, "pool": nc.gpsimd, "dve": nc.vector}
-        x_src = ((xr_words, xr_scales), (xi_words, xi_scales))
-        a_src = ((ar_words, ar_scales), (ai_words, ai_scales))
-        tiles = {}
+        def as_words(ap):
+            return ap.bitcast(I32)
 
-        def move(e, out, in_):
-            if e == "act":
+        def clear(engine, scale_tile):
+            engine.memset(as_words(scale_tile[:].rearrange("p g n -> p (g n)")), 0)
+
+        def load_scale_rows(scale_tile, source, cols, rows):
+            by_row = source[:, :, cols].rearrange("g (q r) n -> r q g n", r=4)
+            for r in rows:
+                nc.sync.dma_start(out=as_words(scale_tile[r:P:32, :, cols]), in_=as_words(by_row[r]))
+
+        def load_x_scales(m, rows):
+            load_scale_rows(x_scales[m], (xr_scales, xi_scales)[m], slice(0, S), rows)
+
+        def load_a_scales(m, g):
+            load_scale_rows(a_loaded_scales[m], (ar_scales, ai_scales)[m], slice(GROUP * g, GROUP * (g + 1)), range(4))
+
+        def load_x(m):
+            source = (xr_words, xi_words)[m].rearrange("g p n t -> p g (n t)")
+            nc.sync.dma_start(out=as_words(x_words[m][:]), in_=as_words(source))
+
+        def load_a(m, g):
+            source = (ar_words, ai_words)[m][:, :, 2 * GROUP * g:2 * GROUP * (g + 1)].rearrange("k p n -> p k n")
+            nc.sync.dma_start(out=as_words(a_loaded[m, g][:]), in_=as_words(source))
+
+        def load_b(m, g, h):
+            source = (br, bi)[m][GROUP * g:GROUP * (g + 1), GROUP * h:GROUP * (h + 1)]
+            by_c = source.rearrange("(a t c) n -> c a t n", t=4, c=4)
+            for c in range(4):
+                nc.sync.dma_start(out=b_rows[m, g, h][c:P:4, :, :], in_=by_c[c])
+
+        clear(nc.gpsimd, a_loaded_scales[IM])
+        clear(nc.vector, x_scales[IM])
+        clear(nc.vector, a_loaded_scales[RE])
+        clear(nc.vector, x_scales[RE])
+        nc.gpsimd.memset(d_rows[:], 0.0)
+        for m in parts:
+            nc.gpsimd.dma_start(out=d_rows[4 * m:4 * m + 4, :, :].rearrange("t g (a c) -> t (g a) c", c=4),
+                                in_=(d_re, d_im)[m].rearrange("(a t c) -> t a c", t=4, c=4))
+        make_identity(nc, identity_bf16[:])
+        nc.scalar.activation(out=identity[:], in_=identity_bf16[:], func=ACT.Copy)
+        load_a_scales(IM, 0)
+        load_x_scales(IM, (0, 1))
+        load_a(IM, 0)
+        load_x(IM)
+        load_x_scales(IM, (2, 3))
+        load_a_scales(RE, 0)
+        load_a(RE, 0)
+        load_x(RE)
+        load_x_scales(RE, range(4))
+        load_b(RE, 0, 0)
+        load_b(IM, 0, 0)
+        load_a(IM, 1)
+        load_a(RE, 1)
+        load_a_scales(IM, 1)
+        load_a_scales(RE, 1)
+        for g, h in ((1, 0), (0, 1), (1, 1)):
+            load_b(RE, g, h)
+            load_b(IM, g, h)
+
+        made = {}
+        free_banks = list(range(8))
+        bank_of = {}
+
+        def take_bank(key):
+            bank_of[key] = free_banks[0]
+            free_banks.remove(bank_of[key])
+            made[key] = psum.tile([P, GROUP], F32, name="bank%d" % bank_of[key])
+            return made[key]
+
+        def give_back(key):
+            free_banks.append(bank_of[key])
+
+        def copy(engine, out, in_):
+            if engine == "S":
                 nc.scalar.copy(out=out, in_=in_)
-            elif e == "dve":
-                nc.vector.tensor_copy(out=out, in_=in_)
             else:
-                nc.gpsimd.tensor_scalar(out=out, in0=in_, scalar1=1.0, scalar2=0.0, op0=ALU.mult, op1=ALU.add)
+                nc.vector.tensor_copy(out=out, in_=in_)
 
-        def interleave(e, out, in_):
-            move(e, out, in_.rearrange("p t n -> p n t"))
+        def interleave(engine, key, name, depth, rows):
+            if engine == "G":
+                made[key] = work.tile([P, PIECE, 4], BF16, name="mixed_on_gpsimd", bufs=1, align_bytes=64)
+                nc.gpsimd.tensor_scalar(out=made[key][:], in0=rows.rearrange("p t n -> p n t"),
+                                        scalar1=1.0, scalar2=0.0, op0=ALU.mult, op1=ALU.add)
+                return
+            made[key] = work.tile([P, PIECE, 4], BF16, name=name, bufs=depth, align_bytes=64)
+            copy(engine, made[key][:].rearrange("p (n i) t -> p n t i", i=4), rows.rearrange("p t (n i) -> p n t i", i=4))
 
         def quantize(words, scales, values):
             nc.vector.quantize_mx(out=words.bitcast(FP8X4), scales=scales, in_=values)
 
-        def first(acc, i, am, xm, start, stop):
+        def first_product(acc, i, a_part, x_part, start, stop):
             g, t = divmod(i, 4)
-            for k in range(2):
+            for k in two:
                 nc.tensor.matmul_mx(
-                    out=acc[:], lhsT=a_words[am][g][:, k, t, :].bitcast(FP4X4), lhsT_scale=a_scales[am][g][:, k, t, :],
-                    rhs=x_words[xm][:, k, :].bitcast(FP8X4), rhs_scale=x_scales[xm][:, k, :],
+                    out=acc[:], lhsT=a_words[a_part, g][:, k, t, :].bitcast(FP4X4), lhsT_scale=a_scales[a_part, g][:, k, t, :],
+                    rhs=x_words[x_part][:, k, :].bitcast(FP8X4), rhs_scale=x_scales[x_part][:, k, :],
                     start=start and k == 0, stop=stop and k == 1)
 
-        def second(acc, u, g, terms):
+        zr_terms = ((RE, RE), (MINUS_IM, IM))
+        zi_terms = ((RE, IM), (IM, RE))
+
+        def second_products(acc, u, g, terms, first_col, width):
             h, j = divmod(u, 4)
-            c, first_row = divmod(P * j, S // CHUNKS[g])
-            rows = slice(first_row, first_row + P)
-            cols = slice(512 * h, 512 * (h + 1))
-            for n, (hm, bm) in enumerate(terms):
+            c, first_state = divmod(P * j, PIECE)
+            states = slice(first_state, first_state + P)
+            cols = slice(GROUP * h + first_col, GROUP * h + first_col + width)
+            for n, (h_part, b_part) in enumerate(terms):
                 nc.tensor.matmul_mx(
-                    out=acc[:], lhsT=h_words[g][:, c, hm, rows].bitcast(FP8X4), lhsT_scale=h_scales[g][:, c, hm, rows],
-                    rhs=b_words[bm][g][:, cols].bitcast(FP8X4), rhs_scale=b_scales[bm][g][:, cols],
+                    out=acc, lhsT=h_words[g, c, h_part][:, states].bitcast(FP8X4), lhsT_scale=h_scales[g, c, h_part][:, states],
+                    rhs=b_words[b_part, g][:, cols].bitcast(FP8X4), rhs_scale=b_scales[b_part, g][:, cols],
                     start=g == 0 and n == 0, stop=g == 1 and n == 1)
 
-        def group_of(u):
-            n = [u in units for units in GROUPS].index(True)
-            return n, u - GROUPS[n][0]
+        def squares_of(u):
+            n = [u in units for units in BATCHES].index(True)
+            if ("squares", n) not in made:
+                made["squares", n] = work.tile([P, len(BATCHES[n]), 2, GROUP], F32, name="squares", bufs=2)
+            return made["squares", n][:, u - BATCHES[n][0], :, :]
 
-        def step(e, kind, a):
-            eng = queues.get(e)
-            if kind == "warm":
-                nc.vector.memset(warm[:], 0.0)
-                nc.scalar.activation(out=warm[:, 1:2], in_=warm[:, 0:1], func=ACT.Square)
-            elif kind == "ident":
-                make_identity(nc, identity[:])
-            elif kind == "zd":
-                eng.memset(d_rows[:], 0.0)
-            elif kind == "ld":
-                m = a[0]
-                eng.dma_start(out=d_rows[4 * m:4 * m + 4, :, :].rearrange("t g (a c) -> t (g a) c", c=4),
-                              in_=(d_re, d_im)[m].rearrange("(a t c) -> t a c", t=4, c=4))
-            elif kind == "d32":
-                nc.vector.tensor_copy(out=d_rows32[:], in_=d_rows[:])
-            elif kind == "dt":
-                tiles["dt"] = bank(a[0])
-                for g in range(2):
-                    nc.tensor.transpose(tiles["dt"][:, P * g:P * (g + 1)], d_rows32[:, g, :], identity[:])
-            elif kind == "dc":
-                turned = tiles["dt"][:, :2 * P].rearrange("p (g c) -> p g c", g=2)
-                nc.vector.tensor_copy(out=d_cols[:, :, 0:8], in_=turned[:, :, 0:8])
-                nc.vector.tensor_scalar(out=d_cols[:, :, 8:12], in0=turned[:, :, 4:8], scalar1=-1.0, scalar2=None, op0=ALU.mult)
-            elif kind == "za":
-                eng.memset(a_raw_scales[a[0]][:].rearrange("p g n -> p (g n)").bitcast(I32), 0)
-            elif kind == "zx":
-                eng.memset(x_scales[a[0]][:].rearrange("p g n -> p (g n)").bitcast(I32), 0)
-            elif kind in ("las", "lxs"):
-                m = a[0]
-                plane, source = (a_raw_scales[m], a_src[m][1]) if kind == "las" else (x_scales[m], x_src[m][1])
-                rows = source.rearrange("g (q r) n -> r q g n", r=4)
-                for r in a[1:]:
-                    eng.dma_start(out=plane[r:P:32, :, :].bitcast(I32), in_=rows[r].bitcast(I32))
-            elif kind == "lx":
-                m = a[0]
-                eng.dma_start(out=x_words[m][:].bitcast(I32),
-                              in_=x_src[m][0].rearrange("g p n t -> p g (n t)").bitcast(I32))
-            elif kind == "la":
-                m, g = a
-                eng.dma_start(out=a_raw[m][g][:].bitcast(I32),
-                              in_=a_src[m][0][:, :, 1024 * g:1024 * (g + 1)].rearrange("k p n -> p k n").bitcast(I32))
-            elif kind == "lb":
-                m, g, h0, h1 = a
-                cols = slice(512 * h0, 512 * h1)
-                rows = (br, bi)[m][512 * g:512 * (g + 1), cols].rearrange("(a t c) n -> c a t n", t=4, c=4)
-                for c in range(4):
-                    eng.dma_start(out=b_raw[m][g][c:P:4, :, cols], in_=rows[c])
-            elif kind == "aw":
-                m, g = a
-                nc.vector.tensor_copy(
-                    out=a_words[m][g][:].bitcast(I32).rearrange("p k t (a j) -> p k t a j", j=2),
-                    in_=a_raw[m][g][:].bitcast(I32).rearrange("p k (a t j) -> p k t a j", t=4, j=2))
-            elif kind == "as":
-                m, g = a
-                nc.vector.tensor_copy(
-                    out=a_scales[m][g][:].bitcast(I32),
-                    in_=a_raw_scales[m][:, :, 512 * g:512 * (g + 1)].bitcast(I32).rearrange("p k (a t) -> p k t a", t=4))
-            elif kind in ("ii", "rr", "ir"):
-                i, n = a
-                tiles[kind, i] = bank(n)
-                first(tiles[kind, i], i, RE if kind == "rr" else IM, IM if kind == "ii" else RE, True, kind != "ir")
-            elif kind == "ri":
-                first(tiles["ir", a[0]], a[0], RE, IM, False, True)
-            elif kind == "a1":
-                tiles["ii_sb", a[0]] = work.tile([P, S], F32, name="ii_sb", bufs=4)
-                nc.scalar.copy(out=tiles["ii_sb", a[0]][:], in_=tiles["ii", a[0]][:])
-            elif kind == "v1":
-                tiles["ur", a[0]] = work.tile([P, S], F32, name="ur", bufs=3)
-                nc.vector.tensor_tensor(out=tiles["ur", a[0]][:], in0=tiles["rr", a[0]][:], in1=tiles["ii_sb", a[0]][:],
-                                        op=ALU.subtract)
-            elif kind in ("a2", "a3"):
-                i = a[0]
-                g, t = divmod(i, 4)
-                c = t if kind == "a2" else 4 + t
-                tiles[kind, i] = work.tile([P, S], F32, name="ur_" + kind, bufs=3)
-                nc.scalar.activation(out=tiles[kind, i][:], in_=tiles["ur", i][:], func=ACT.Copy, scale=d_cols[:, g, c:c + 1])
-            elif kind in ("v2", "v3"):
-                i = a[0]
-                g, t = divmod(i, 4)
-                m, c, other = (RE, 8 + t, "a2") if kind == "v2" else (IM, t, "a3")
-                nc.vector.scalar_tensor_tensor(out=h_rows[g][:, m, t, :], in0=tiles["ir", i][:],
-                                               scalar=d_cols[:, g, c:c + 1], in1=tiles[other, i][:],
-                                               op0=ALU.mult, op1=ALU.add)
-            elif kind == "b":
-                m, g, h, q = a
-                if ("b", m, g, h) not in tiles:
-                    tiles["b", m, g, h] = work.tile([P, 512, 4], BF16, name="b_grouped", bufs=3, align_bytes=64)
-                c0 = 512 * h + 256 * q
-                interleave(e, tiles["b", m, g, h][:, 256 * q:256 * (q + 1), :], b_raw[m][g][:, :, c0:c0 + 256])
-            elif kind == "bq":
-                m, g, h = a
-                cols = slice(512 * h, 512 * (h + 1))
-                quantize(b_words[m][g][:, cols], b_scales[m][g][:, cols], tiles["b", m, g, h][:].rearrange("p n t -> p (n t)"))
-            elif kind == "h":
-                g, c, m, q = a
-                width = min(256, S // CHUNKS[g])
-                s0 = c * (S // CHUNKS[g]) + width * q
-                interleave(e, h_grouped[g][:, c, m, width * q:width * (q + 1), :], h_rows[g][:, m, :, s0:s0 + width])
-            elif kind == "hn":
-                g, c = a
-                nc.vector.tensor_scalar(out=h_grouped[g][:, c, NEG_IM, :, :], in0=h_grouped[g][:, c, IM, :, :],
-                                        scalar1=-1.0, scalar2=None, op0=ALU.mult)
-            elif kind == "hq":
-                g, c = a
-                quantize(h_words[g][:, c, 0:2, :].rearrange("p m s -> p (m s)"),
-                         h_scales[g][:, c, 0:2, :].rearrange("p m s -> p (m s)"),
-                         h_grouped[g][:, c, 0:2, :, :].rearrange("p m s t -> p (m s t)"))
-            elif kind == "hqn":
-                g, c = a
-                quantize(h_words[g][:, c, NEG_IM, :], h_scales[g][:, c, NEG_IM, :],
-                         h_grouped[g][:, c, NEG_IM, :, :].rearrange("p s t -> p (s t)"))
-            elif kind in ("zr", "zi"):
-                u, g = a[0], a[1]
-                if g == 0:
-                    tiles[kind, u] = bank(a[2])
-                second(tiles[kind, u], u, g, [(RE, RE), (NEG_IM, IM)] if kind == "zr" else [(RE, IM), (IM, RE)])
-            elif kind in ("sr", "si"):
-                n, place = group_of(a[0])
-                if ("sq", n) not in tiles:
-                    tiles["sq", n] = work.tile([P, len(GROUPS[n]), 2, 512], F32, name="sq", bufs=2)
-                nc.scalar.activation(out=tiles["sq", n][:, place, 0 if kind == "sr" else 1, :],
-                                     in_=tiles["z" + kind[1], a[0]][:], func=ACT.Square)
-            elif kind == "add":
-                n = a[0]
-                tiles["y", n] = work.tile([P, len(GROUPS[n]), 512], F32, name="y", bufs=3)
-                nc.vector.tensor_tensor(out=tiles["y", n][:], in0=tiles["sq", n][:, :, 0, :], in1=tiles["sq", n][:, :, 1, :],
-                                        op=ALU.add)
-            elif kind == "sy":
-                n = a[0]
-                h, j = divmod(GROUPS[n][0], 4)
-                rows = out_0[P * j:P * (j + len(GROUPS[n])), 512 * h:512 * (h + 1)]
-                eng.dma_start(out=rows.rearrange("(u s) n -> s u n", s=P), in_=tiles["y", n][:])
-            elif kind == "cast":
-                n = a[0]
-                tiles["pairs", n] = work.tile([P, len(GROUPS[n]), 2, P, 2], BF16, name="y_pairs", bufs=3)
-                move(e, tiles["pairs", n][:], tiles["y", n][:].rearrange("s u (p w e) -> s u w p e", w=2, e=2))
-            elif kind == "turn":
-                n = a[1]
-                tiles["turned", n] = bank(a[0])
-                words = tiles["pairs", n][:].rearrange("s u w p e -> s (u w p e)").bitcast(F32)
-                for c in range(2 * len(GROUPS[n])):
-                    nc.tensor.transpose(tiles["turned", n][:, P * c:P * (c + 1)], words[:, P * c:P * (c + 1)], identity[:])
-            elif kind == "rg":
-                n = a[0]
-                count = len(GROUPS[n])
-                tiles["yg", n] = work.tile([P, count * P * 4], BF16, name="y_grouped", bufs=3, align_bytes=64)
-                move(e, tiles["yg", n][:].bitcast(F32).rearrange("p (u s w) -> p u s w", w=2, s=P),
-                     tiles["turned", n][:, :2 * P * count].rearrange("p (u w s) -> p u s w", w=2, s=P))
-            elif kind == "yq":
-                n = a[0]
-                h, j = divmod(GROUPS[n][0], 4)
-                cols = slice(P * j, P * (j + len(GROUPS[n])))
-                quantize(y_words[h][:, cols], y_scales[h][:, cols], tiles["yg", n][:])
-            elif kind == "sw":
-                h, j0, j1 = a
-                cols = slice(P * j0, P * j1)
-                eng.dma_start(out=out_1[h, :, cols, :].rearrange("p m t -> p (m t)").bitcast(I32),
-                              in_=y_words[h][:, cols].bitcast(I32))
-            elif kind == "ss":
-                h, j0, j1 = a[:3]
-                cols = slice(P * j0, P * j1)
-                rows = out_2[h].rearrange("(q r) m -> r q m", r=4)
-                for r in a[3:]:
-                    eng.dma_start(out=rows[r][:, cols].bitcast(I32), in_=y_scales[h][r:P:32, cols].bitcast(I32))
-            else:
-                raise ValueError(kind)
+        def batch_place(n):
+            h, j = divmod(BATCHES[n][0], 4)
+            return h, slice(P * j, P * (j + len(BATCHES[n])))
 
-        for item in PROGRAM.split():
-            fields = item.split(".")
-            step(fields[0], fields[1], [int(c) for c in fields[2]] if len(fields) > 2 else [])
+        def a_order(item, engine):
+            nc.vector.tensor_copy(out=as_words(a_words[item][:]).rearrange("p k t (a j) -> p k t a j", j=2),
+                                  in_=as_words(a_loaded[item][:]).rearrange("p k (a t j) -> p k t a j", t=4, j=2))
+
+        def as_order(item, engine):
+            m, g = item
+            source = as_words(a_loaded_scales[m][:, :, GROUP * g:GROUP * (g + 1)])
+            nc.vector.tensor_copy(out=as_words(a_scales[item][:]), in_=source.rearrange("p k (a t) -> p k t a", t=4))
+
+        def d_f32(item, engine):
+            nc.scalar.activation(out=d_rows_f32[:], in_=d_rows[:], func=ACT.Copy)
+
+        def d_turn(item, engine):
+            turned = take_bank("d")
+            for g in two:
+                nc.tensor.transpose(turned[:, P * g:P * (g + 1)], d_rows_f32[:, g, :], identity[:])
+
+        def d_out(item, engine):
+            turned = made["d"][:, :2 * P].rearrange("p (g m t) -> p g m t", g=2, t=4)
+            nc.vector.tensor_copy(out=d_columns[:, :, RE:IM + 1, :], in_=turned[:, :, RE:IM + 1, :])
+            nc.vector.tensor_scalar(out=d_columns[:, :, MINUS_IM, :], in0=turned[:, :, IM, :],
+                                    scalar1=-1.0, scalar2=None, op0=ALU.mult)
+            give_back("d")
+
+        def d_of(i, part):
+            g, t = divmod(i, 4)
+            return d_columns[:, g, part, t:t + 1]
+
+        def ii(i, engine):
+            first_product(take_bank(("ii", i)), i, IM, IM, True, True)
+
+        def rr(i, engine):
+            first_product(take_bank(("rr", i)), i, RE, RE, True, True)
+
+        def ir(i, engine):
+            first_product(take_bank(("ui", i)), i, IM, RE, True, False)
+
+        def ri(i, engine):
+            first_product(made["ui", i], i, RE, IM, False, True)
+
+        def ii_out(i, engine):
+            made["ii_out", i] = work.tile([P, S], F32, name="ii_out", bufs=4)
+            nc.scalar.copy(out=made["ii_out", i][:], in_=made["ii", i][:])
+            give_back(("ii", i))
+
+        def ur(i, engine):
+            made["ur", i] = work.tile([P, S], F32, name="ur")
+            nc.vector.tensor_tensor(out=made["ur", i][:], in0=made["rr", i][:], in1=made["ii_out", i][:], op=ALU.subtract)
+            give_back(("rr", i))
+
+        def scaled_ur(i, part):
+            made["ur_d", part, i] = work.tile([P, S], F32, name="ur_d%d" % part)
+            nc.scalar.activation(out=made["ur_d", part, i][:], in_=made["ur", i][:], func=ACT.Copy, scale=d_of(i, part))
+
+        def h_row(i, part, factor):
+            g, t = divmod(i, 4)
+            nc.vector.scalar_tensor_tensor(out=h_rows[part, g][:, t, :], in0=made["ui", i][:], scalar=d_of(i, factor),
+                                           in1=made["ur_d", part, i][:], op0=ALU.mult, op1=ALU.add)
+            if ("ui_read", i) in made:
+                give_back(("ui", i))
+            made["ui_read", i] = True
+
+        def b_mix(item, engine):
+            m, g, h, q = item
+            interleave(engine, ("b", item), "b_mixed", 4, b_rows[m, g, h][:, :, PIECE * q:PIECE * (q + 1)])
+
+        def b_q(item, engine):
+            m, g, h, q = item
+            cols = slice(GROUP * h + PIECE * q, GROUP * h + PIECE * (q + 1))
+            quantize(b_words[m, g][:, cols], b_scales[m, g][:, cols], made["b", item][:].rearrange("p n t -> p (n t)"))
+
+        def h_mix(item, part, engine):
+            g, c = item
+            interleave(engine, ("h", g, c, part), "h_mixed%d%d%d" % (g, c, part), 1,
+                       h_rows[part, g][:, :, PIECE * c:PIECE * (c + 1)])
+
+        def negate(item, engine):
+            g, c = item
+            made["h", g, c, MINUS_IM] = work.tile([P, PIECE, 4], BF16, name="h_negated", bufs=2, align_bytes=64)
+            nc.vector.tensor_scalar(out=made["h", g, c, MINUS_IM][:], in0=made["h", g, c, IM][:],
+                                    scalar1=-1.0, scalar2=None, op0=ALU.mult)
+
+        def h_q(item, part):
+            g, c = item
+            quantize(h_words[g, c, part][:], h_scales[g, c, part][:], made["h", g, c, part][:].rearrange("p s t -> p (s t)"))
+
+        def z_open(name, u, terms):
+            second_products(take_bank((name, u))[:], u, 0, terms, 0, GROUP)
+
+        def z_close(name, u, terms):
+            second_products(made[name, u][:], u, 1, terms, 0, GROUP)
+
+        def z_square(name, u, part):
+            nc.scalar.activation(out=squares_of(u)[:, part, :], in_=made[name, u][:], func=ACT.Square)
+            give_back((name, u))
+
+        def zi_half(q, engine):
+            acc = take_bank(("zi_half", q))
+            for g in two:
+                second_products(acc[:, :PIECE], LAST_UNIT, g, zi_terms, PIECE * q, PIECE)
+
+        def half_sq(q, engine):
+            nc.scalar.activation(out=squares_of(LAST_UNIT)[:, IM, PIECE * q:PIECE * (q + 1)],
+                                 in_=made["zi_half", q][:, :PIECE], func=ACT.Square)
+            give_back(("zi_half", q))
+
+        def pairs_tile(n):
+            if ("pairs", n) not in made:
+                made["pairs", n] = work.tile([P, len(BATCHES[n]), 2, P, 2], BF16, name="y_pairs")
+            return made["pairs", n]
+
+        def half_pairs(q, engine):
+            zr_sq, zi_sq = (squares_of(LAST_UNIT)[:, m, PIECE * q:PIECE * (q + 1)].rearrange("s (p w e) -> s w p e", w=2, e=2)
+                            for m in parts)
+            places = slice(PIECE // 4 * q, PIECE // 4 * (q + 1))
+            nc.vector.tensor_tensor(out=pairs_tile(LAST_BATCH)[:, 0, :, places, :], in0=zr_sq, in1=zi_sq, op=ALU.add)
+
+        def y_sum(n, engine):
+            made["y", n] = work.tile([P, len(BATCHES[n]), GROUP], F32, name="y")
+            nc.vector.tensor_tensor(out=made["y", n][:], in0=made["squares", n][:, :, RE, :],
+                                    in1=made["squares", n][:, :, IM, :], op=ALU.add)
+
+        def y_out(n, engine):
+            h, states = batch_place(n)
+            target = out_0[states, GROUP * h:GROUP * (h + 1)].rearrange("(u s) n -> s u n", s=P)
+            nc.sync.dma_start(out=target, in_=made["y", n][:])
+
+        def pairs(n, engine):
+            copy(engine, pairs_tile(n)[:], made["y", n][:].rearrange("s u (p w e) -> s u w p e", w=2, e=2))
+
+        def y_turn(n, engine):
+            turned = take_bank(("turned", n))
+            words = made["pairs", n][:].rearrange("s u w p e -> s (u w p e)").bitcast(F32)
+            for c in range(2 * len(BATCHES[n])):
+                nc.tensor.transpose(turned[:, P * c:P * (c + 1)], words[:, P * c:P * (c + 1)], identity[:])
+
+        def regroup(n, engine):
+            units = len(BATCHES[n])
+            made["y_mixed", n] = work.tile([P, units * P * 4], BF16, name="y_mixed", align_bytes=64)
+            copy(engine, made["y_mixed", n][:].bitcast(F32).rearrange("p (u s w) -> p u s w", w=2, s=P),
+                 made["turned", n][:, :2 * P * units].rearrange("p (u w s) -> p u s w", w=2, s=P))
+            give_back(("turned", n))
+
+        def y_q(n, engine):
+            h, states = batch_place(n)
+            quantize(y_words[h][:, states], y_scales[h][:, states], made["y_mixed", n][:])
+
+        def codes_out(item, engine):
+            h, states = item
+            nc.sync.dma_start(out=as_words(out_1[h, :, states, :].rearrange("p m t -> p (m t)")),
+                              in_=as_words(y_words[h][:, states]))
+
+        def scales_out(item, engine):
+            h, r = item
+            queue = nc.scalar if engine == "S" else nc.sync
+            queue.dma_start(out=as_words(out_2[h].rearrange("(q r) m -> r q m", r=4)[r]), in_=as_words(y_scales[h][r:P:32, :]))
+
+        tiles_1 = range(8)
+        a_items = [(m, g) for g in two for m in (IM, RE)]
+        b_items = [(m, g, h, q) for h in two for g in two for m in parts for q in two]
+        batches = range(len(BATCHES))
+        steps = {
+            "a_order": (a_order, a_items), "as_order": (as_order, a_items),
+            "d_f32": (d_f32, [0]), "d_turn": (d_turn, [0]), "d_out": (d_out, [0]),
+            "ii": (ii, tiles_1), "rr": (rr, tiles_1), "ir": (ir, tiles_1), "ri": (ri, tiles_1),
+            "ii_out": (ii_out, tiles_1), "ur": (ur, tiles_1),
+            "ur_dr": (lambda i, engine: scaled_ur(i, RE), tiles_1), "ur_di": (lambda i, engine: scaled_ur(i, IM), tiles_1),
+            "hr": (lambda i, engine: h_row(i, RE, MINUS_IM), tiles_1), "hi": (lambda i, engine: h_row(i, IM, RE), tiles_1),
+            "b_mix": (b_mix, b_items), "b_q": (b_q, b_items),
+            "hr_mix": (lambda item, engine: h_mix(item, RE, engine), h_pieces),
+            "hi_mix": (lambda item, engine: h_mix(item, IM, engine), h_pieces),
+            "negate": (negate, h_pieces),
+            "hr_q": (lambda item, engine: h_q(item, RE), h_pieces), "hi_q": (lambda item, engine: h_q(item, IM), h_pieces),
+            "neg_q": (lambda item, engine: h_q(item, MINUS_IM), h_pieces),
+            "zr_open": (lambda u, engine: z_open("zr", u, zr_terms), range(8)),
+            "zi_open": (lambda u, engine: z_open("zi", u, zi_terms), range(LAST_UNIT)),
+            "zr_close": (lambda u, engine: z_close("zr", u, zr_terms), range(8)),
+            "zi_close": (lambda u, engine: z_close("zi", u, zi_terms), range(LAST_UNIT)),
+            "zr_sq": (lambda u, engine: z_square("zr", u, RE), range(8)),
+            "zi_sq": (lambda u, engine: z_square("zi", u, IM), range(LAST_UNIT)),
+            "zi_half": (zi_half, two), "half_sq": (half_sq, two), "half_pairs": (half_pairs, two),
+            "y_sum": (y_sum, batches), "y_out": (y_out, batches), "pairs": (pairs, batches),
+            "y_turn": (y_turn, batches), "regroup": (regroup, batches), "y_q": (y_q, batches),
+            "codes_out": (codes_out, [(0, slice(0, S)), (1, slice(0, 3 * P)), (1, slice(3 * P, S))]),
+            "scales_out": (scales_out, [(h, r) for h in two for r in range(4)]),
+        }
+        taken = {kind: 0 for kind in steps}
+        for word in ORDER.split():
+            kind, engine = (word + ":").split(":")[:2]
+            step, items = steps[kind]
+            step(items[taken[kind]], engine)
+            taken[kind] += 1

@@ -26,19 +26,19 @@ LAST_UNIT = 7
 LAST_BATCH = len(BATCHES) - 1
 
 ORDER = """
-a_order as_order d_f32 ii as_order ii a_order ii_out ii d_turn d_out ii_out ii_out rr ii ur rr ii_out rr b_mix:G
-ur ur_di rr ur ur_dr ir ur_dr ri ur ur_dr ir b_q ur_di hi ri b_mix:G ur_di hr ir b_mix:S hr ri hi ir ur_dr
-a_order ri as_order ur_di a_order ii b_q b_mix:S as_order ii b_q hr b_mix:G rr ii_out hi ii ii_out hi ii ii_out
-ur rr hi_mix:S hr ir b_q ir b_q ur_di rr hr_mix:V ur_dr ri ur b_mix:G ii_out ri ur ur_di rr hi ur_dr ir hr_q
-hi_mix:S ir hi_q b_q zi_open negate hr_mix:G hr ur_di zi_open ur ri ur_dr hr ri ur_di negate ur_dr neg_q hr_q
-b_mix:S zr_open hi zr_open hr b_mix:S b_mix:G hi hi hi_q hi_mix:S hr zi_open neg_q b_q zr_open hr_mix:V hr_mix:S
-zi_open b_q hr_q zr_open hi_mix:S hi_q negate zi_close hr_q neg_q zi_close b_mix:V b_mix:S zr_close b_q zi_sq
-zr_close hi_q negate zr_sq zi_close b_q zi_sq neg_q zi_close b_mix:V b_mix:S zr_close b_q zr_close b_q b_mix:V
-zr_sq zi_open b_mix:V zr_sq zi_open zi_sq b_mix:V zi_open zi_sq zr_open b_q b_q zr_sq zr_open b_q b_q zr_open
-y_sum zr_close zi_close y_sum zr_close y_out zr_sq zi_close zi_sq pairs:V zr_close y_out zr_sq pairs:V zi_close
-zi_sq zr_open zr_sq y_sum y_turn zi_sq y_turn regroup:S zr_close y_sum y_out regroup:S zi_half pairs:V y_out
+as_order a_order ii as_order ii a_order ii_out ii ii_out ii d_f32 ii_out rr ii_out rr ur d_turn rr d_out b_mix:S
+b_mix:G ur ir ur ri ur_di rr b_q ur_dr b_q ir hi ur_di b_mix:G ri ur ur_dr ir hr ur_di ri hi ur_dr ir a_order
+b_mix:S ri as_order a_order ii b_q as_order ur_dr ii hi b_mix:G ur_di ii hr ii_out rr hr ii_out rr hr ii_out ir
+ur hr_mix:S ri b_q b_q ii hi ur_dr rr b_mix:V ir ur_di hi_mix:G ur ir ii_out hr ir ur_dr ur rr ur_di hr_q ri
+ur_dr negate ri hi_q ur_di neg_q ri hr_mix:G ur b_mix:S zr_open hi zr_open hi ur_di zi_open b_q ur_dr zi_open
+hr_q hr hi_mix:S b_mix:G hr hi b_mix:S hi b_q hi_mix:S hi_q hr zi_open negate hi_mix:S hr_mix:V zi_open neg_q
+hr_q hr_mix:S zr_open b_q hi_q zr_open negate b_mix:S negate zi_close neg_q zi_close b_q hr_q zr_close hi_q
+b_mix:V b_mix:S zr_close zi_close neg_q zr_sq b_mix:V zi_close zi_sq b_q zr_close zi_sq b_q zr_close b_q zi_sq
+b_mix:V zr_open zr_sq b_mix:V zr_open zr_sq b_q zi_open zr_sq b_q zi_open b_mix:V zi_sq zi_open b_q b_q zr_open
+y_sum zi_close zr_close y_sum zi_close y_out zi_sq zr_close zr_sq pairs:V zr_close y_out zi_sq pairs:V zi_close
+zr_sq y_turn zr_sq y_sum y_turn zi_sq zr_open regroup:S zr_close y_sum y_out regroup:S zi_half pairs:V y_out
 zr_sq zi_half y_q half_sq y_q y_turn pairs:V half_sq scales_out half_pairs scales_out regroup:S scales_out
-y_turn codes_out half_pairs scales_out y_sum regroup:S y_turn y_q regroup:S y_out y_q y_q codes_out codes_out
+y_turn scales_out half_pairs codes_out y_sum regroup:S y_turn y_q regroup:S y_out y_q y_q codes_out codes_out
 scales_out scales_out scales_out:S scales_out:S
 """
 

from contextlib import ExitStack

import concourse.mybir as mybir
from concourse.masks import make_identity

F32 = mybir.dt.float32
BF16 = mybir.dt.bfloat16
I32 = mybir.dt.int32
U32 = mybir.dt.uint32
U8 = mybir.dt.uint8
FP8X4 = mybir.dt.float8_e4m3fn_x4
FP4X4 = mybir.dt.float4_e2m1fn_x4
ACT = mybir.ActivationFunctionType
ALU = mybir.AluOpType

P = 128
S = 512
D = 1024
FLOPS = 8 * 2 * S * D * D
GROUP = 512
PIECE = 256
RE, IM, MINUS_IM = 0, 1, 2

BATCHES = ((0, 1), (2, 3), (4, 5), (6,), (7,))
LAST_UNIT = 7
LAST_BATCH = len(BATCHES) - 1

ORDER = """
as_order a_order ii as_order ii a_order ii_out ii ii_out ii d_f32 ii_out rr ii_out rr ur d_turn rr d_out b_mix:S
b_mix:G ur ir ur ri ur_di rr b_q ur_dr b_q ir hi ur_di b_mix:G ri ur ur_dr ir hr ur_di ri hi ur_dr ir a_order
b_mix:S ri as_order a_order ii b_q as_order ur_dr ii hi b_mix:G ur_di ii hr ii_out rr hr ii_out rr hr ii_out ir
ur hr_mix:S ri b_q b_q ii hi ur_dr rr b_mix:V ir ur_di hi_mix:G ur ir ii_out hr ir ur_dr ur rr ur_di hr_q ri
ur_dr negate ri hi_q ur_di neg_q ri hr_mix:G ur b_mix:S zr_open hi zr_open hi ur_di zi_open b_q ur_dr zi_open
hr_q hr hi_mix:S b_mix:G hr hi b_mix:S hi b_q hi_mix:S hi_q hr zi_open negate hi_mix:S hr_mix:V zi_open neg_q
hr_q hr_mix:S zr_open b_q hi_q zr_open negate b_mix:S negate zi_close neg_q zi_close b_q hr_q zr_close hi_q
b_mix:V b_mix:S zr_close zi_close neg_q zr_sq b_mix:V zi_close zi_sq b_q zr_close zi_sq b_q zr_close b_q zi_sq
b_mix:V zr_open zr_sq b_mix:V zr_open zr_sq b_q zi_open zr_sq b_q zi_open b_mix:V zi_sq zi_open b_q b_q zr_open
y_sum zi_close zr_close y_sum zi_close y_out zi_sq zr_close zr_sq pairs:V zr_close y_out zi_sq pairs:V zi_close
zr_sq y_turn zr_sq y_sum y_turn zi_sq zr_open regroup:S zr_close y_sum y_out regroup:S zi_half pairs:V y_out
zr_sq zi_half y_q half_sq y_q y_turn pairs:V half_sq scales_out half_pairs scales_out regroup:S scales_out
y_turn scales_out half_pairs codes_out y_sum regroup:S y_turn y_q regroup:S y_out y_q y_q codes_out codes_out
scales_out scales_out scales_out:S scales_out:S
"""


def tile_complex_layers_intensity_planes_h2_kernel(
    tc, xr_words, xr_scales, xi_words, xi_scales, ar_words, ar_scales, ai_words, ai_scales,
    d_re, d_im, br, bi, out_0, out_1, out_2,
):
    nc = tc.nc
    with ExitStack() as ctx:
        keep = ctx.enter_context(tc.tile_pool(name="keep", bufs=1))
        work = ctx.enter_context(tc.tile_pool(name="work", bufs=3))
        psum = ctx.enter_context(tc.psum_pool(name="psum", bufs=1))
        ctx.enter_context(tc.manual_schedule())

        def kept(name, shape, dtype):
            return keep.tile(shape, dtype, name=name, align_bytes=64)

        parts = (RE, IM)
        two = range(2)
        part_groups = [(m, g) for m in parts for g in two]
        h_pieces = [(g, c) for g in two for c in two]
        h_keys = [(g, c, m) for g, c in h_pieces for m in (RE, IM, MINUS_IM)]
        x_words = [kept("x_words%d" % m, [P, 2, S], U32) for m in parts]
        x_scales = [kept("x_scales%d" % m, [P, 2, S], U8) for m in parts]
        a_loaded = {k: kept("a_loaded%d%d" % k, [P, 2, 2 * GROUP], U8) for k in part_groups}
        a_loaded_scales = [kept("a_loaded_scales%d" % m, [P, 2, D], U8) for m in parts]
        a_words = {k: kept("a_words%d%d" % k, [P, 2, 4, 2 * P], U8) for k in part_groups}
        a_scales = {k: kept("a_scales%d%d" % k, [P, 2, 4, P], U8) for k in part_groups}
        b_rows = {(m, g, h): kept("b_rows%d%d%d" % (m, g, h), [P, 4, GROUP], BF16) for m, g in part_groups for h in two}
        b_words = {k: kept("b_words%d%d" % k, [P, D], U32) for k in part_groups}
        b_scales = {k: kept("b_scales%d%d" % k, [P, D], U8) for k in part_groups}
        h_rows = {k: kept("h_rows%d%d" % k, [P, 4, S], BF16) for k in part_groups}
        h_words = {k: kept("h_words%d%d%d" % k, [P, PIECE], U32) for k in h_keys}
        h_scales = {k: kept("h_scales%d%d%d" % k, [P, PIECE], U8) for k in h_keys}
        y_words = [kept("y_words%d" % h, [P, S], U32) for h in two]
        y_scales = [kept("y_scales%d" % h, [P, S], U8) for h in two]
        identity_bf16 = kept("identity_bf16", [P, P], BF16)
        identity = kept("identity", [P, P], F32)
        d_rows = kept("d_rows", [P, 2, P], BF16)
        d_rows_f32 = kept("d_rows_f32", [P, 2, P], F32)
        d_columns = kept("d_columns", [P, 2, 3, 4], F32)

        def as_words(ap):
            return ap.bitcast(I32)

        def clear(engine, scale_tile):
            engine.memset(as_words(scale_tile[:].rearrange("p g n -> p (g n)")), 0)

        def load_scale_rows(scale_tile, source, cols, rows):
            by_row = source[:, :, cols].rearrange("g (q r) n -> r q g n", r=4)
            for r in rows:
                nc.sync.dma_start(out=as_words(scale_tile[r:P:32, :, cols]), in_=as_words(by_row[r]))

        def load_x_scales(m, rows):
            load_scale_rows(x_scales[m], (xr_scales, xi_scales)[m], slice(0, S), rows)

        def load_a_scales(m, g):
            load_scale_rows(a_loaded_scales[m], (ar_scales, ai_scales)[m], slice(GROUP * g, GROUP * (g + 1)), range(4))

        def load_x(m):
            source = (xr_words, xi_words)[m].rearrange("g p n t -> p g (n t)")
            nc.sync.dma_start(out=as_words(x_words[m][:]), in_=as_words(source))

        def load_a(m, g):
            source = (ar_words, ai_words)[m][:, :, 2 * GROUP * g:2 * GROUP * (g + 1)].rearrange("k p n -> p k n")
            nc.sync.dma_start(out=as_words(a_loaded[m, g][:]), in_=as_words(source))

        def load_b(m, g, h):
            source = (br, bi)[m][GROUP * g:GROUP * (g + 1), GROUP * h:GROUP * (h + 1)]
            by_c = source.rearrange("(a t c) n -> c a t n", t=4, c=4)
            for c in range(4):
                nc.sync.dma_start(out=b_rows[m, g, h][c:P:4, :, :], in_=by_c[c])

        clear(nc.gpsimd, a_loaded_scales[IM])
        clear(nc.vector, x_scales[IM])
        clear(nc.vector, a_loaded_scales[RE])
        clear(nc.vector, x_scales[RE])
        nc.gpsimd.memset(d_rows[:], 0.0)
        for m in parts:
            nc.gpsimd.dma_start(out=d_rows[4 * m:4 * m + 4, :, :].rearrange("t g (a c) -> t (g a) c", c=4),
                                in_=(d_re, d_im)[m].rearrange("(a t c) -> t a c", t=4, c=4))
        make_identity(nc, identity_bf16[:])
        nc.scalar.activation(out=identity[:], in_=identity_bf16[:], func=ACT.Copy)
        load_a_scales(IM, 0)
        load_x_scales(IM, (0, 1))
        load_a(IM, 0)
        load_x(IM)
        load_x_scales(IM, (2, 3))
        load_a_scales(RE, 0)
        load_a(RE, 0)
        load_x(RE)
        load_x_scales(RE, range(4))
        load_b(RE, 0, 0)
        load_b(IM, 0, 0)
        load_a(IM, 1)
        load_a(RE, 1)
        load_a_scales(IM, 1)
        load_a_scales(RE, 1)
        for g, h in ((1, 0), (0, 1), (1, 1)):
            load_b(RE, g, h)
            load_b(IM, g, h)

        made = {}
        free_banks = list(range(8))
        bank_of = {}

        def take_bank(key):
            bank_of[key] = free_banks[0]
            free_banks.remove(bank_of[key])
            made[key] = psum.tile([P, GROUP], F32, name="bank%d" % bank_of[key])
            return made[key]

        def give_back(key):
            free_banks.append(bank_of[key])

        def copy(engine, out, in_):
            if engine == "S":
                nc.scalar.copy(out=out, in_=in_)
            else:
                nc.vector.tensor_copy(out=out, in_=in_)

        def interleave(engine, key, name, depth, rows):
            if engine == "G":
                made[key] = work.tile([P, PIECE, 4], BF16, name="mixed_on_gpsimd", bufs=1, align_bytes=64)
                nc.gpsimd.tensor_scalar(out=made[key][:], in0=rows.rearrange("p t n -> p n t"),
                                        scalar1=1.0, scalar2=0.0, op0=ALU.mult, op1=ALU.add)
                return
            made[key] = work.tile([P, PIECE, 4], BF16, name=name, bufs=depth, align_bytes=64)
            copy(engine, made[key][:].rearrange("p (n i) t -> p n t i", i=4), rows.rearrange("p t (n i) -> p n t i", i=4))

        def quantize(words, scales, values):
            nc.vector.quantize_mx(out=words.bitcast(FP8X4), scales=scales, in_=values)

        def first_product(acc, i, a_part, x_part, start, stop):
            g, t = divmod(i, 4)
            for k in two:
                nc.tensor.matmul_mx(
                    out=acc[:], lhsT=a_words[a_part, g][:, k, t, :].bitcast(FP4X4), lhsT_scale=a_scales[a_part, g][:, k, t, :],
                    rhs=x_words[x_part][:, k, :].bitcast(FP8X4), rhs_scale=x_scales[x_part][:, k, :],
                    start=start and k == 0, stop=stop and k == 1)

        zr_terms = ((RE, RE), (MINUS_IM, IM))
        zi_terms = ((RE, IM), (IM, RE))

        def second_products(acc, u, g, terms, first_col, width):
            h, j = divmod(u, 4)
            c, first_state = divmod(P * j, PIECE)
            states = slice(first_state, first_state + P)
            cols = slice(GROUP * h + first_col, GROUP * h + first_col + width)
            for n, (h_part, b_part) in enumerate(terms):
                nc.tensor.matmul_mx(
                    out=acc, lhsT=h_words[g, c, h_part][:, states].bitcast(FP8X4), lhsT_scale=h_scales[g, c, h_part][:, states],
                    rhs=b_words[b_part, g][:, cols].bitcast(FP8X4), rhs_scale=b_scales[b_part, g][:, cols],
                    start=g == 0 and n == 0, stop=g == 1 and n == 1)

        def squares_of(u):
            n = [u in units for units in BATCHES].index(True)
            if ("squares", n) not in made:
                made["squares", n] = work.tile([P, len(BATCHES[n]), 2, GROUP], F32, name="squares", bufs=2)
            return made["squares", n][:, u - BATCHES[n][0], :, :]

        def batch_place(n):
            h, j = divmod(BATCHES[n][0], 4)
            return h, slice(P * j, P * (j + len(BATCHES[n])))

        def a_order(item, engine):
            nc.vector.tensor_copy(out=as_words(a_words[item][:]).rearrange("p k t (a j) -> p k t a j", j=2),
                                  in_=as_words(a_loaded[item][:]).rearrange("p k (a t j) -> p k t a j", t=4, j=2))

        def as_order(item, engine):
            m, g = item
            source = as_words(a_loaded_scales[m][:, :, GROUP * g:GROUP * (g + 1)])
            nc.vector.tensor_copy(out=as_words(a_scales[item][:]), in_=source.rearrange("p k (a t) -> p k t a", t=4))

        def d_f32(item, engine):
            nc.scalar.activation(out=d_rows_f32[:], in_=d_rows[:], func=ACT.Copy)

        def d_turn(item, engine):
            turned = take_bank("d")
            for g in two:
                nc.tensor.transpose(turned[:, P * g:P * (g + 1)], d_rows_f32[:, g, :], identity[:])

        def d_out(item, engine):
            turned = made["d"][:, :2 * P].rearrange("p (g m t) -> p g m t", g=2, t=4)
            nc.vector.tensor_copy(out=d_columns[:, :, RE:IM + 1, :], in_=turned[:, :, RE:IM + 1, :])
            nc.vector.tensor_scalar(out=d_columns[:, :, MINUS_IM, :], in0=turned[:, :, IM, :],
                                    scalar1=-1.0, scalar2=None, op0=ALU.mult)
            give_back("d")

        def d_of(i, part):
            g, t = divmod(i, 4)
            return d_columns[:, g, part, t:t + 1]

        def ii(i, engine):
            first_product(take_bank(("ii", i)), i, IM, IM, True, True)

        def rr(i, engine):
            first_product(take_bank(("rr", i)), i, RE, RE, True, True)

        def ir(i, engine):
            first_product(take_bank(("ui", i)), i, IM, RE, True, False)

        def ri(i, engine):
            first_product(made["ui", i], i, RE, IM, False, True)

        def ii_out(i, engine):
            made["ii_out", i] = work.tile([P, S], F32, name="ii_out", bufs=4)
            nc.scalar.copy(out=made["ii_out", i][:], in_=made["ii", i][:])
            give_back(("ii", i))

        def ur(i, engine):
            made["ur", i] = work.tile([P, S], F32, name="ur")
            nc.vector.tensor_tensor(out=made["ur", i][:], in0=made["rr", i][:], in1=made["ii_out", i][:], op=ALU.subtract)
            give_back(("rr", i))

        def scaled_ur(i, part):
            made["ur_d", part, i] = work.tile([P, S], F32, name="ur_d%d" % part)
            nc.scalar.activation(out=made["ur_d", part, i][:], in_=made["ur", i][:], func=ACT.Copy, scale=d_of(i, part))

        def h_row(i, part, factor):
            g, t = divmod(i, 4)
            nc.vector.scalar_tensor_tensor(out=h_rows[part, g][:, t, :], in0=made["ui", i][:], scalar=d_of(i, factor),
                                           in1=made["ur_d", part, i][:], op0=ALU.mult, op1=ALU.add)
            if ("ui_read", i) in made:
                give_back(("ui", i))
            made["ui_read", i] = True

        def b_mix(item, engine):
            m, g, h, q = item
            interleave(engine, ("b", item), "b_mixed", 4, b_rows[m, g, h][:, :, PIECE * q:PIECE * (q + 1)])

        def b_q(item, engine):
            m, g, h, q = item
            cols = slice(GROUP * h + PIECE * q, GROUP * h + PIECE * (q + 1))
            quantize(b_words[m, g][:, cols], b_scales[m, g][:, cols], made["b", item][:].rearrange("p n t -> p (n t)"))

        def h_mix(item, part, engine):
            g, c = item
            interleave(engine, ("h", g, c, part), "h_mixed%d%d%d" % (g, c, part), 1,
                       h_rows[part, g][:, :, PIECE * c:PIECE * (c + 1)])

        def negate(item, engine):
            g, c = item
            made["h", g, c, MINUS_IM] = work.tile([P, PIECE, 4], BF16, name="h_negated", bufs=2, align_bytes=64)
            nc.vector.tensor_scalar(out=made["h", g, c, MINUS_IM][:], in0=made["h", g, c, IM][:],
                                    scalar1=-1.0, scalar2=None, op0=ALU.mult)

        def h_q(item, part):
            g, c = item
            quantize(h_words[g, c, part][:], h_scales[g, c, part][:], made["h", g, c, part][:].rearrange("p s t -> p (s t)"))

        def z_open(name, u, terms):
            second_products(take_bank((name, u))[:], u, 0, terms, 0, GROUP)

        def z_close(name, u, terms):
            second_products(made[name, u][:], u, 1, terms, 0, GROUP)

        def z_square(name, u, part):
            nc.scalar.activation(out=squares_of(u)[:, part, :], in_=made[name, u][:], func=ACT.Square)
            give_back((name, u))

        def zi_half(q, engine):
            acc = take_bank(("zi_half", q))
            for g in two:
                second_products(acc[:, :PIECE], LAST_UNIT, g, zi_terms, PIECE * q, PIECE)

        def half_sq(q, engine):
            nc.scalar.activation(out=squares_of(LAST_UNIT)[:, IM, PIECE * q:PIECE * (q + 1)],
                                 in_=made["zi_half", q][:, :PIECE], func=ACT.Square)
            give_back(("zi_half", q))

        def pairs_tile(n):
            if ("pairs", n) not in made:
                made["pairs", n] = work.tile([P, len(BATCHES[n]), 2, P, 2], BF16, name="y_pairs")
            return made["pairs", n]

        def half_pairs(q, engine):
            zr_sq, zi_sq = (squares_of(LAST_UNIT)[:, m, PIECE * q:PIECE * (q + 1)].rearrange("s (p w e) -> s w p e", w=2, e=2)
                            for m in parts)
            places = slice(PIECE // 4 * q, PIECE // 4 * (q + 1))
            nc.vector.tensor_tensor(out=pairs_tile(LAST_BATCH)[:, 0, :, places, :], in0=zr_sq, in1=zi_sq, op=ALU.add)

        def y_sum(n, engine):
            made["y", n] = work.tile([P, len(BATCHES[n]), GROUP], F32, name="y")
            nc.vector.tensor_tensor(out=made["y", n][:], in0=made["squares", n][:, :, RE, :],
                                    in1=made["squares", n][:, :, IM, :], op=ALU.add)

        def y_out(n, engine):
            h, states = batch_place(n)
            target = out_0[states, GROUP * h:GROUP * (h + 1)].rearrange("(u s) n -> s u n", s=P)
            nc.sync.dma_start(out=target, in_=made["y", n][:])

        def pairs(n, engine):
            copy(engine, pairs_tile(n)[:], made["y", n][:].rearrange("s u (p w e) -> s u w p e", w=2, e=2))

        def y_turn(n, engine):
            turned = take_bank(("turned", n))
            words = made["pairs", n][:].rearrange("s u w p e -> s (u w p e)").bitcast(F32)
            for c in range(2 * len(BATCHES[n])):
                nc.tensor.transpose(turned[:, P * c:P * (c + 1)], words[:, P * c:P * (c + 1)], identity[:])

        def regroup(n, engine):
            units = len(BATCHES[n])
            made["y_mixed", n] = work.tile([P, units * P * 4], BF16, name="y_mixed", align_bytes=64)
            copy(engine, made["y_mixed", n][:].bitcast(F32).rearrange("p (u s w) -> p u s w", w=2, s=P),
                 made["turned", n][:, :2 * P * units].rearrange("p (u w s) -> p u s w", w=2, s=P))
            give_back(("turned", n))

        def y_q(n, engine):
            h, states = batch_place(n)
            quantize(y_words[h][:, states], y_scales[h][:, states], made["y_mixed", n][:])

        def codes_out(item, engine):
            h, states = item
            nc.sync.dma_start(out=as_words(out_1[h, :, states, :].rearrange("p m t -> p (m t)")),
                              in_=as_words(y_words[h][:, states]))

        def scales_out(item, engine):
            h, r = item
            queue = nc.scalar if engine == "S" else nc.sync
            queue.dma_start(out=as_words(out_2[h].rearrange("(q r) m -> r q m", r=4)[r]), in_=as_words(y_scales[h][r:P:32, :]))

        tiles_1 = range(8)
        a_items = [(m, g) for g in two for m in (IM, RE)]
        b_items = [(m, g, h, q) for h in two for g in two for m in parts for q in two]
        batches = range(len(BATCHES))
        steps = {
            "a_order": (a_order, a_items), "as_order": (as_order, a_items),
            "d_f32": (d_f32, [0]), "d_turn": (d_turn, [0]), "d_out": (d_out, [0]),
            "ii": (ii, tiles_1), "rr": (rr, tiles_1), "ir": (ir, tiles_1), "ri": (ri, tiles_1),
            "ii_out": (ii_out, tiles_1), "ur": (ur, tiles_1),
            "ur_dr": (lambda i, engine: scaled_ur(i, RE), tiles_1), "ur_di": (lambda i, engine: scaled_ur(i, IM), tiles_1),
            "hr": (lambda i, engine: h_row(i, RE, MINUS_IM), tiles_1), "hi": (lambda i, engine: h_row(i, IM, RE), tiles_1),
            "b_mix": (b_mix, b_items), "b_q": (b_q, b_items),
            "hr_mix": (lambda item, engine: h_mix(item, RE, engine), h_pieces),
            "hi_mix": (lambda item, engine: h_mix(item, IM, engine), h_pieces),
            "negate": (negate, h_pieces),
            "hr_q": (lambda item, engine: h_q(item, RE), h_pieces), "hi_q": (lambda item, engine: h_q(item, IM), h_pieces),
            "neg_q": (lambda item, engine: h_q(item, MINUS_IM), h_pieces),
            "zr_open": (lambda u, engine: z_open("zr", u, zr_terms), range(8)),
            "zi_open": (lambda u, engine: z_open("zi", u, zi_terms), range(LAST_UNIT)),
            "zr_close": (lambda u, engine: z_close("zr", u, zr_terms), range(8)),
            "zi_close": (lambda u, engine: z_close("zi", u, zi_terms), range(LAST_UNIT)),
            "zr_sq": (lambda u, engine: z_square("zr", u, RE), range(8)),
            "zi_sq": (lambda u, engine: z_square("zi", u, IM), range(LAST_UNIT)),
            "zi_half": (zi_half, two), "half_sq": (half_sq, two), "half_pairs": (half_pairs, two),
            "y_sum": (y_sum, batches), "y_out": (y_out, batches), "pairs": (pairs, batches),
            "y_turn": (y_turn, batches), "regroup": (regroup, batches), "y_q": (y_q, batches),
            "codes_out": (codes_out, [(0, slice(0, S)), (1, slice(0, 3 * P)), (1, slice(3 * P, S))]),
            "scales_out": (scales_out, [(h, r) for h in two for r in range(4)]),
        }
        taken = {kind: 0 for kind in steps}
        for word in ORDER.split():
            kind, engine = (word + ":").split(":")[:2]
            step, items = steps[kind]
            step(items[taken[kind]], engine)
            taken[kind] += 1
